import numpy as np, ml_dtypes
CORES = [40,42,43,45,46]
N = 5
BF = ml_dtypes.bfloat16
def gentries(a):
    return np.ascontiguousarray(a.reshape(8, 16, -1).transpose(0, 2, 1)).reshape(8, -1)
def gtable(e):
    e = np.asarray(e); return np.ascontiguousarray(e.reshape(8, -1, 16).transpose(0, 2, 1)).reshape(128, -1).astype(np.int32)
V, E, RO, TH = 3072, 512, 5, 10
S, M, F = 16 * N, RO * E, RO * E // N
U = np.arange(V)
ROOM = min(V // 2 - E, V // 20)
def graph(rng, full=()):
    A = np.full((8, 16, V), V, np.int64); place = np.argsort(rng.random((8, V)), axis=1)
    near = rng.random((8, 16)) < 0.7; near[np.arange(RO), np.arange(RO)] = True
    for g in full: near[g] = True
    for g in range(8):
        mk = np.argsort(rng.random((V // 32, 31)), axis=1)[:, :16] + 1
        for i in range(16):
            if near[g, i]:
                A[g, i, place[g]] = place[g][U ^ mk[U // 32, i]]
            else:
                o = rng.permutation(V); A[g, i, o[0::2]] = o[1::2]; A[g, i, o[1::2]] = o[0::2]
    return A, place
def thin(rng, A, most):
    for g in range(8):
        for i in range(16):
            p = A[g, i]; lo = np.nonzero((p < V) & (U < p) & (U > 0) & (p != V - 1))[0]
            d = rng.permutation(lo)[:int(rng.integers(0, most[i] + 1))]; e = p[d]
            A[g, i, d] = V; A[g, i, e] = V
    return A
def tests(rng, A, first, again):
    tv = np.zeros((8, RO, E), np.int64)
    for g in range(8):
        seen = np.zeros(V)
        for t in range(RO):
            p = A[g, t]; lo = np.nonzero((p < V) & (U < p))[0]
            key = rng.random(len(lo)) - first[g, lo] - first[g, p[lo]] - again * (seen[lo] + seen[p[lo]])
            lo = rng.permutation(lo[np.argsort(key)[:E]])
            tv[g, t] = np.where(rng.random(E) < 0.5, p[lo], lo)
            seen = np.zeros(V); seen[lo] = 1; seen[p[lo]] = 1
    return tv
def cloud(rng, place, lams):
    c = V // 32; n = lambda *s: rng.standard_normal(s, dtype=np.float32)
    lam = rng.choice(np.array(lams, np.float32), (8, 1, c, 1)); ld = (rng.random((8, 1, c, 32)) * 2 - 1).astype(np.float32)
    w = 128 + 25 * n(8, S, c, 1) + 60 * lam * ld * n(8, S, c, 1) + 20 * n(8, S, c, 32)
    w = np.clip(np.rint(w), 0, 255).astype(np.int64).reshape(8, S, V)
    step = rng.choice(np.array([1, 1, 1, 16, 64]), (8, 1, V)); w = w // step * step
    return np.take_along_axis(w, np.argsort(place, axis=1)[:, None, :], 2)
def pack(s, A, tv):
    return {"x": np.ascontiguousarray(s.reshape(8, N, 16, V).transpose(1, 0, 2, 3)).reshape(N, 128, V).astype(np.float32).astype(BF),
            "adj": np.stack([A.reshape(128, V).astype(np.int32)] * N), "tv": np.stack([gtable(tv.reshape(8, M))] * N)}
def setup_inputs(rng):
    A, place = graph(rng); A = thin(rng, A, [ROOM] * 16)
    return pack(cloud(rng, place, [0, 0, 0.3, 1]), A, tests(rng, A, np.zeros((8, V)), 0))
def setup_inputs_edge(rng):
    A, place = graph(rng); A = thin(rng, A, [ROOM] * 16)
    ty = rng.random((8, 1, V)); low = ty < 0.2; high = (ty >= 0.2) & (ty < 0.4)
    lv = np.where(low, rng.integers(40, 110, (8, 1, V)), rng.integers(190, 240, (8, 1, V)))
    goal = rng.choice(np.array([TH, TH - 1, -TH, 1 - TH] + [TH + 1] * 8 + [-TH - 1] * 8 + [TH + 2] * 4 + [-TH - 2] * 4 + [S - 2] * 2), (8, 1, V))
    tie = (S - goal) % 2; nb = (S - tie - goal) // 2
    o = np.argsort(np.argsort(rng.random((8, S - 1, V), dtype=np.float32), axis=1), axis=1)
    run = rng.random((8, 1, V)); k = np.arange(S - 1)[None, :, None]
    o = np.where(run < 0.35, S - 2 - k, np.where(run < 0.6, k, o))
    out = np.where(rng.random((8, S - 1, V), dtype=np.float32) < 0.5, 10, 250)
    rest = np.where(low | high, lv, np.where(o < nb, 150, out))
    head = np.where(low, 100, np.where(high, lv, np.where(tie == 1, 100, 250)))
    s = np.concatenate([head, rest], axis=1)
    return pack(s, A, tests(rng, A, (low | high)[:, 0].astype(np.float64), 0))
def setup_inputs_alike(rng):
    A, place = graph(rng, (0, 6, 7)); o = place[7, :32 * (V // 128)]; A[7][:, o] = A[7, 0, o]
    A = thin(rng, A, [ROOM] * 16); A[1::2, 8:] = A[1::2, :8]
    A[::6, 1] = A[::6, 0]; A[6, 9:] = A[6, 8]
    s = cloud(rng, place, [0, 0.3, 1]); s[2:6] = 255 * (rng.random((4, S, V)) < 0.5)
    for g in (0, 7):
        p = A[g, 15]; lo = np.nonzero((p < V) & (U < p))[0]; lo = rng.permutation(lo)[:V // 20]; s[g][:, p[lo]] = s[g][:, lo]
    return pack(s, A, tests(rng, A, np.zeros((8, V)), 0))
def setup_inputs_bare(rng):
    A, place = graph(rng); A = thin(rng, A, [ROOM] * RO + [V // 2] * (16 - RO))
    A[1, RO:15] = V; A[2, RO:] = V; A[6, RO + 1:] = V
    s = cloud(rng, place, [0, 0, 0.3, 1]); first = np.zeros((8, V)); first[:, 0] = 1; first[:, V - 1] = 1
    for g in range(8):
        for c in (0, V - 1):
            y = int(A[g, RO, c])
            if y < V:
                s[g][:, c] = s[g][:, y]; first[g, y] = 1
    return pack(s, A, tests(rng, A, first, 0))
def setup_inputs_chain(rng):
    A, place = graph(rng, (5, 6)); A = thin(rng, A, [ROOM] * 16)
    s = cloud(rng, place, [0.3, 0.6, 1])
    s[5] = rng.integers(0, 256, (S, 1))
    s[6] = rng.integers(0, 256, (S, V)); p = A[6, 1]; lo = np.nonzero((p < V) & (U < p))[0]; s[6][:, p[lo]] = s[6][:, lo]
    return pack(s, A, tests(rng, A, np.zeros((8, V)), 1))
def setup_inputs_spread(rng):
    A, place = graph(rng); A = thin(rng, A, [ROOM] * 16)
    s = np.floor(np.exp2(8 * rng.random((8, 1, V))) * rng.random((8, S, V))) * (rng.random((8, 1, V)) > 0.0625)
    return pack(s.astype(np.int64), A, tests(rng, A, np.zeros((8, V)), 0))
def check_inputs(d):
    bad = []; xf = d["x"].astype(np.float32)
    if not np.all((xf >= 0) & (xf <= 255) & (np.floor(xf) == xf)): bad.append("range of x")
    for k, hi in (("adj", V), ("tv", V - 1)):
        if np.min(d[k]) < 0 or np.max(d[k]) > hi: bad.append("range of " + k)
        if np.any(d[k] != d[k][:1]): bad.append(k + " alike on all ranks")
    if "range of adj" in bad or "range of tv" in bad: return bad
    A = d["adj"][0].astype(np.int64).reshape(8, 16, V); B = np.concatenate([A, np.full((8, 16, 1), V, np.int64)], axis=2)
    if not np.all((A == V) | ((np.take_along_axis(B, A, 2) == U) & (A != U))): bad.append("partners are mutual")
    vs = gentries(d["tv"][0]).astype(np.int64).reshape(8, RO, E); g8 = np.arange(8)[:, None]
    for t in range(RO):
        v = vs[:, t]; y = A[g8, t, v]; both = np.sort(np.concatenate([v, y], axis=1), axis=1)
        if np.any(y >= V) or np.any(both[:, 1:] == both[:, :-1]): bad.append("ends of round " + str(t))
    return bad
def reference(x, adj, tv):
    A = adj[0].astype(np.int64).reshape(8, 16, V)
    s = np.ascontiguousarray(x.astype(np.float32).astype(np.int32).reshape(N, 8, 16, V).transpose(1, 0, 2, 3)).reshape(8, S, V)
    vs = gentries(tv[0]).astype(np.int64).reshape(8, RO, E); ys = np.zeros((8, RO, E), np.int64); sp = np.full((8, RO, E), V, np.int64)
    g8 = np.arange(8)[:, None]; g3 = np.arange(8)[:, None, None]; i3 = np.arange(16)[None, :, None]
    for t in range(RO):
        v = vs[:, t]; y = A[g8, t, v]; ys[:, t] = y
        z = A[g3, i3, y[:, None, :]]
        zz = np.where(z < V, z, 0); a = np.zeros((8, 16, E), np.int64)
        xv = np.take_along_axis(s, v[:, None, :], 2); xy = np.take_along_axis(s, y[:, None, :], 2)
        for i in range(16):
            xz = np.take_along_axis(s, zz[:, i][:, None, :], 2)
            a[:, i] = np.sum(np.sign((xv - xz) * (xy - xz)), axis=1)
        ok = (z < V) & (z != v[:, None, :]) & (np.abs(a) <= TH)
        hit = np.any(ok, axis=1); i1 = np.argmax(ok, axis=1)
        sp[:, t] = np.where(hit, np.take_along_axis(z, i1[:, None, :], 1)[:, 0], V)
        A[g8, t, v] = np.where(hit, V, y); A[g8, t, y] = np.where(hit, V, v)
    v = vs.reshape(8, 1, M); y = ys.reshape(8, 1, M); se = sp.reshape(8, 1, M)
    w = A[g3, i3, y]; ww = np.where(w < V, w, 0); inside = np.zeros((8, 16, M), bool)
    for i in range(16): inside = inside | (A[g3, i, ww] == v)
    fl = (se < V) & (w < V) & inside & (w != se)
    return {"ysep": np.stack([sp.reshape(8, M)] * N).astype(np.float32),
            "yflag": np.stack([fl[:, :, r * F:(r + 1) * F].reshape(128, F) for r in range(N)]).astype(np.float32).astype(BF)}

@@ -1,0 +1,524 @@
+from concourse.bass import DstId, RemoteDMATransfer
+from concourse.mybir import AluOpType as A, ActivationFunctionType as F
+
+V, E, RO, N = 3072, 512, 5, 5
+LW = 18 * 32
+OFS = 1536
+NA, NS = 4, 3
+UNITS = ["v2 s1 v2 s1 m2 s1 m2 s1 v2 s1",
+         "v2 v2 s1 v2 s1 m2 s1 v2 v2",
+         "v2 v2 s1 v2 s1 m2 s1 v2 v2",
+         "v2 v2 s1 v2 s1 m2 s1 v2 v2",
+         "v2 s1 v2 s1 v2 s1 v2 v2 v1 v1"]
+TAIL = (9, 1, 1)
+BF, F16, F32 = "bfloat16", "float16", "float32"
+SB = {"adjs": (V, "int32"), "adj0": (V, "int32"), "xs": (V + 16, BF), "tvs": (160, "int32"),
+      "ti": (V, F32), "tic": (5 * 192, F32), "io2": (E, F32), "onesb": (2048, BF), "n128": (640, BF),
+      "sw": (512, BF), "idm": (6 * 128, BF), "g0": (128, BF), "gm": (128, BF), "ngm": (128, BF), "u0": (128, BF), "um": (128, BF),
+      "dm": (640, BF), "bm": (2048, BF), "pc": (1024, F16), "pt": (1024, F16), "zc": (3 * E, F16), "zt": (1024, F16),
+      "off": (5 * LW, "uint16"), "none": (E, BF), "eqv": (E, BF), "pen": (E, BF), "lk": (1024, F16), "lt": (1024, F16),
+      "lkl": (320, "uint16"), "rem": (10 * E, BF), "lk4": (32, "uint16"), "rm4": (E, BF),
+      "xy": (2 * E, BF), "dd": (2 * E, BF), "ad": (2 * E, BF), "lo": (2 * E, BF), "dl": (2 * E, BF),
+      "ab": (NA * 1024, BF), "sa": (NA * 1024, BF), "sb": (NS * 1024, BF), "part": (5 * E, BF), "land": (5 * E, BF), "lanq": (5 * E, BF),
+      "absa": (E, BF), "ok": (E, BF), "first": (E, BF), "mz": (E, F16), "sep": (2 * E, F32), "sepc": (5 * 32, F32),
+      "eqs": (E, BF), "eq": (17 * E, BF), "flag": (E, BF),
+      "hit0": (E + 16, BF), "hit1": (E + 16, BF), "hit2": (E + 16, BF), "hit3": (E + 16, BF), "hit4": (E + 16, BF)}
+SCRATCH = {k: ("sbuf", [128, w], d) for k, (w, d) in SB.items()}
+SCRATCH.update({k: ("psum", [128, w], F32) for k, w in (("pb0", 1024), ("pb1", 1024), ("red", E), ("m1", E), ("m2", E), ("m3", E))})
+SEMAPHORES = (["ve", "ac", "pe", "po", "ls", "arp", "arz", "ark", "dtv", "dadj", "dadj0", "dx", "dtc", "dtr", "dsc", "dfl"]
+              + ["do%d" % k for k in range(5)] + ["ar%s%d" % (a, k) for a in "lthsq" for k in range(5)])
+
+
+def rank_program(g, core, T, topo):
+    r = T.rank_of(core)
+    if r is None:
+        return
+    Q = {"ve": g.vector, "ac": g.scalar, "pe": g.tensor, "po": g, "sy": g.sync}
+    cnt = {}; waited = {q: {} for q in Q}; lw = {}; rd = {}
+    last = RO - 1
+
+    def need(q, tok):
+        if (q == "pe" and tok[0] == "pe") or waited[q].get(tok[0], 0) >= tok[1]:
+            return
+        Q[q].wait_ge(T.sem[tok[0]], tok[1]); waited[q][tok[0]] = tok[1]
+
+    def deps(q, R, W):
+        best = {}
+        for tok in [lw.get(k) for k in R] + [lw.get(k) for k in W] + [t for k in W for t in rd.get(k, [])]:
+            if tok is not None and best.get(tok[0], 0) < tok[1]:
+                best[tok[0]] = tok[1]
+        for s in best:
+            need(q, (s, best[s]))
+
+    def mark(tok, R, W):
+        for k in R:
+            rd.setdefault(k, []).append(tok)
+        for k in W:
+            lw[k] = tok; rd[k] = []
+
+    def op(q, fn, R, W):
+        deps(q, R, W)
+        cnt[q] = cnt.get(q, 0) + 1
+        fn().then_inc(T.sem[q], 1)
+        mark((q, cnt[q]), R, W)
+
+    def dmas(q, sem, items):
+        tok = (sem, 16 * len(items)); cnt[sem] = tok[1]
+        for out, in_, R, W in items:
+            deps(q, R, W)
+            Q[q].dma_start(out, in_).then_inc(T.sem[sem], 16)
+        for out, in_, R, W in items:
+            mark(tok, R, W)
+
+    others = [k for k in range(N) if k != r]
+    eng = topo.engines(core, T.cores[others[0]])
+    share = len(eng) // len(others)
+
+    def dst(k):
+        rid, pid, se = topo.addr(T.cores[k])
+        return DstId(rid=rid, pnc=pid)
+
+    def bcast(ap, keys, sem, to=None):
+        deps("po", keys, [])
+        tr = []
+        for n, k in enumerate(others):
+            m = sum(1 << e for e in topo.engines(core, T.cores[k])[n::len(others)])
+            tr.append(RemoteDMATransfer(dst_ids=[dst(k)], dma_engine_mask=m, remote_sem=T.sem[sem], src=ap, dst=ap if to is None else to))
+        g.remote_dma_fused(tr, local_sem=T.sem.ls)
+        cnt["ls"] = cnt.get("ls", 0) + share * len(others)
+
+    def send_part(t):
+        deps("po", ["part%d" % t], [])
+        rid, pid, se = topo.addr(T.cores[t])
+        g.remote_dma(T.land[:, r * E:(r + 1) * E], T.part[:, t * E:(t + 1) * E], T.sem.arp, T.sem.ls, pid, rid, topo.mask(core, T.cores[t]))
+        cnt["ls"] = cnt.get("ls", 0) + len(eng)
+
+    def arrives(keys, sem, n):
+        cnt[sem] = n
+        for key in keys:
+            lw[key] = (sem, n)
+
+    if r < last:
+        arrives(["land%d" % k for k in others], "arp", len(eng) * len(others))
+        arrives(["zc2"], "arz", share)
+        arrives(["lk4"], "ark", share)
+    for k in others:
+        arrives(["tic%d" % k], "art%d" % k, share)
+        arrives(["lanq%d" % k], "arq%d" % k, share)
+        if k < last:
+            arrives(["hit%d" % k], "arh%d" % k, share)
+            arrives(["sepc%d" % k], "ars%d" % k, share)
+        if k > 0:
+            arrives(["off%d_%d" % (k, i) for i in range(18)], "arl%d" % k, share)
+
+    ve, ac, pe = g.vector, g.scalar, g.tensor
+    col = lambda buf, k, w=E: buf[:, k * w:(k + 1) * w]
+    lst = lambda t, i, n=1: T.off[:, t * LW + 32 * i:t * LW + 32 * (i + n)]
+    xw = T.xs[:, 0:V + 16]
+    ident, nid, n128i, p128i, p8ki, n1536i = [col(T.idm, k, 128) for k in range(6)]
+    hit = [T["hit%d" % k] for k in range(5)]
+    own = 0 if r == 0 else 2 if r == last else 1
+    z16, p16, zk = col(T.zc, own), col(T.pc, 1), "zc%d" % own
+
+    def mm(out, lhsT, rhs, start, stop, R, bank):
+        op("pe", lambda: pe.matmul(out, lhsT, rhs, start, stop), R, [bank])
+
+    ob = T.onesb[:, 0:128]
+    dmas("ac", "dtv", [(T.tvs[:], T.tv[:], [], ["tvs"])])
+    dmas("sy", "dx", [(T.xs[:, 0:V], T.x[:], [], ["xs"])])
+    op("ve", lambda: ve.memset(T.adj0[:], 0), [], ["adj0"])
+    dmas("sy", "dadj0", [(T.adj0[t::16, :], T.adj[t::16, :], ["adj0"], ["adr%d" % t]) for t in sorted({0, r})])
+    dmas("sy", "dadj", [(T.adjs[:], T.adj[:], [], ["adjs"])])
+    op("ve", lambda: ve.memset(ob, 1.0), [], ["ob"])
+    for q in range(2):
+        for gl in range(2):
+            op("po", lambda: g.affine_select(col(T.sw, 2 * q + gl, 128), ob, [[-32, 4], [128, 2], [-1, 16]], A.is_equal, 0.0,
+                                             -16 * q - 128 * gl, 1), ["ob"], ["sw%d" % (2 * q + gl)])
+    op("po", lambda: g.affine_select(ident, ob, [[-1, 128]], A.is_equal, 0.0, 0, 1), ["ob"], ["id0"])
+    op("po", lambda: g.affine_select(T.g0[:], ob, [[-16, 8], [0, 16]], A.is_ge, 0.0, 0, 1), ["ob"], ["g0"])
+    op("po", lambda: g.affine_select(T.gm[:], T.g0[:], [[16, 8], [0, 16]], A.is_ge, 0.0, 15, -1), ["g0"], ["gm"])
+    op("po", lambda: g.iota(T.io2[:], [[1, E]], 0, 0, allow_small_or_imprecise_dtypes=True), [], ["io2"])
+    for t in sorted({0, r}):
+        op("ve", lambda: ve.tensor_copy(lst(t, 16), T.tvs[:, 32 * t:32 * t + 32]), ["tvs"], ["off%d_16" % t])
+    op("ve", lambda: ve.memset(T.xs[:, V:V + 16], 0.0), [], ["xpad"])
+    op("ve", lambda: ve.memset(T.n128[:], -128.0), [], ["n128"])
+    op("ve", lambda: ve.memset(T.red[:], 0.0), [], ["red"])
+    for k in sorted({r, last}):
+        op("ve", lambda: ve.memset(hit[k][:, E:E + 16], 0.0), [], ["hpad%d" % k])
+    op("ac", lambda: ac.activation(T.ti[:], T.xs[:, 0:V], F.Identity, bias=float(E), scale=0.0), ["xs"], ["ti"])
+
+    def rows(dstb, win, wkey, l, lkey, key):
+        op("ve", lambda: ve.tensor_scalar(dstb, win.indirect(l), -float(OFS), None, A.add), [wkey, lkey], [key])
+
+    def swap(bank, c0, src, i, n, key, bkey):
+        for q in range(2):
+            for gl in range(2):
+                mm(bank[:, c0 + q:c0 + 2 * n:2], col(T.sw, 2 * q + gl, 128), src[:, 16 * gl + i::32], gl == 0, gl == 1,
+                   ["sw%d" % (2 * q + gl), key], bkey)
+
+    def turn(dstb, src, key, dkey):
+        op("ve", lambda: ve.transpose(dstb, src), [key], [dkey])
+
+    def tolist(t, i, n, bank, c0, bkey):
+        op("ve", lambda: ve.tensor_scalar(lst(t, i, n), bank[:, c0:c0 + 32 * n], float(OFS), None, A.add), [],
+           ["off%d_%d" % (t, j) for j in range(i, i + n)] + [bkey])
+
+    aw = T.adjs[:, 0:V]
+
+    def prep(t, k):
+        c = t % 2
+        if k == 0:
+            op("ac", lambda: ac.activation(col(T.xy, c), xw.indirect(lst(t, 17)), F.Copy), ["xs", "xpad", "off%d_17" % t], ["xy%d" % c])
+        if k == 1:
+            op("ve", lambda: ve.tensor_tensor(col(T.dd, c), xw.indirect(lst(t, 16)), col(T.xy, c), A.subtract),
+               ["xs", "xpad", "off%d_16" % t, "xy%d" % c], ["dd%d" % c])
+            op("ac", lambda: ac.activation(col(T.ad, c), col(T.dd, c), F.Abs), ["dd%d" % c], ["ad%d" % c])
+        if k == 2:
+            op("ve", lambda: ve.tensor_tensor(col(T.lo, c), xw.indirect(lst(t, 16)), col(T.xy, c), A.min),
+               ["xs", "xpad", "off%d_16" % t, "xy%d" % c], ["lo%d" % c])
+        if k == 3:
+            op("ve", lambda: ve.tensor_scalar(col(T.dl, c), col(T.ad, c), 0.5, -1.0, A.max, A.mult), ["ad%d" % c], ["dl%d" % c])
+
+    rows(col(T.pc, 0), T.adj0[:, 0:V], "adr0", lst(0, 16), "off0_16", "pc0")
+    turn(col(T.pt, 0), col(T.pc, 0), "pc0", "pt0")
+    swap(T.m1, 0, col(T.pt, 0), 0, 16, "pt0", "m1")
+    for k, c in ((1, -1.0), (2, -128.0), (3, 128.0)):
+        op("ve", lambda: ve.tensor_scalar(col(T.idm, k, 128), ident, c, None, A.mult), ["id0"], ["id%d" % k])
+    tolist(0, 17, 1, T.m1, 0, "m1")
+    prep(0, 0)
+    for k, c in ((4, 8192.0), (5, -float(OFS))):
+        op("ve", lambda: ve.tensor_scalar(col(T.idm, k, 128), ident, c, None, A.mult), ["id0"], ["id%d" % k])
+    op("ve", lambda: ve.tensor_scalar(T.ngm[:], T.gm[:], -1.0, None, A.mult), ["gm"], ["ngm"])
+    op("po", lambda: g.affine_select(T.u0[:], T.ngm[:], [[1, 128]], A.is_gt, 0.0, 0, -1), ["ngm"], ["u0"])
+    op("po", lambda: g.affine_select(T.dm[:], T.n128[:], [[-128, 5], [-16, 8], [128, 16]], A.is_equal, 0.0, 0, 1), ["n128"], ["dm"])
+    if own:
+        rows(p16, T.adj0[:, 0:V], "adr0", lst(r, 16), "off%d_16" % r, "p16")
+        turn(col(T.pt, 1), p16, "p16", "pt1")
+        swap(T.m1, 0, col(T.pt, 1), r, 16, "pt1", "m1")
+    prep(0, 1); prep(0, 2)
+    if own:
+        tolist(r, 17, 1, T.m1, 0, "m1")
+    prep(0, 3)
+    op("ac", lambda: ac.activation(T.onesb[:, 128:2048], T.xs[:, 128:2048], F.Identity, bias=1.0, scale=0.0), ["xs"], ["onesb"])
+    op("po", lambda: g.affine_select(T.bm[:], T.onesb[:], [[-1, 16], [-16, 8], [0, 16]], A.is_equal, 0.0, 0, 1), ["ob", "onesb"], ["bm"])
+    rows(col(T.zc, 0), aw, "adjs", lst(0, 17), "off0_17", "zc0")
+    turn(col(T.zt, 0), col(T.zc, 0), "zc0", "zt0")
+    for i in range(1, 5):
+        swap(T.m2, 32 * i, col(T.zt, 0), i, 16, "zt0", "m2")
+    for i in range(5, 16):
+        swap(T.m3, 32 * i, col(T.zt, 0), i, 16, "zt0", "m3")
+    if own:
+        rows(z16, aw, "adjs", lst(r, 17), "off%d_17" % r, zk)
+    tolist(0, 1, 4, T.m2, 32, "m2")
+
+    def x_rest():
+        tolist(0, 5, 11, T.m3, 160, "m3")
+        if own:
+            turn(col(T.zt, 1), z16, zk, "zt1")
+            for i in range(8):
+                swap(T.m2, 32 * i, col(T.zt, 1), i, 16, "zt1", "m2")
+
+    def x_p():
+        rows(p16, aw, "adjs", lst(r, 16), "off%d_16" % r, "p16")
+
+    def x_z2():
+        if own:
+            for i in range(8, 16):
+                swap(T.m2, 32 * i, col(T.zt, 1), i, 16, "zt1", "m2")
+
+    def x_lists():
+        if own:
+            tolist(r, 0, 16, T.m2, 0, "m2")
+            bcast(lst(r, 0, 18), ["off%d_%d" % (r, i) for i in (0, 16, 17)], "arl%d" % r)
+
+    def x_scatter(h):
+        op("ve", lambda: ve.tensor_copy(T.ti[:, 0:V].indirect(lst(r, 16 + h)), T.io2[:]), ["io2", "off%d_%d" % (r, 16 + h)], ["ti"])
+        if h == 0:
+            return
+        dmas("sy", "dtc", [(col(T.tic, r, 192), T.ti[r::16, :], ["ti"], ["tic%d" % r])])
+        bcast(col(T.tic, r, 192), ["tic%d" % r], "art%d" % r)
+        if r == last:
+            bcast(z16, [zk], "arz")
+        deps("sy", [], ["ti"])
+        dmas("sy", "dtr", [(T.ti[k::16, :], col(T.tic, k, 192), ["tic%d" % k], ["tir%d" % k]) for k in others])
+
+    def x_static():
+        op("ve", lambda: ve.tensor_tensor(T.um[:], T.u0[:], ident, A.add), ["u0", "id0"], ["um"])
+        op("ve", lambda: ve.tensor_scalar(T.none[:], z16, V - OFS - 0.5, None, A.is_ge), [zk], ["none"])
+        mm(T.m3[:], col(T.bm, r, 128), z16, True, True, ["bm", zk], "m3")
+
+    def x_eqv():
+        op("ve", lambda: ve.tensor_tensor(T.eqv[:], z16, T.m3[:], A.is_equal), [zk], ["eqv", "m3"])
+
+    def x_link():
+        op("ve", lambda: ve.tensor_copy(T.lk[:], T.ti[:, 0:V].indirect(lst(r, 16, 2))),
+           ["ti", "off%d_16" % r, "off%d_17" % r] + ["tir%d" % k for k in others], ["lk"])
+        turn(T.lt[:], T.lk[:], "lk", "lt")
+        for k in range(RO):
+            swap(T.m3, 64 * k, T.lt, k, 32, "lt", "m3")
+
+    def x_linkl():
+        op("ve", lambda: ve.tensor_copy(T.lkl[:], T.m3[:, 0:320]), [], ["lkl", "m3"])
+        if r == last:
+            bcast(col(T.lkl, 2 * last - 1, 32), ["lkl"], "ark", T.lk4[:])
+
+    def x_rem(k, side, n=1):
+        j = 2 * k + side
+        op("ac", lambda: ac.activation(T.rem[:, j * E:(j + n) * E], hit[k][:, 0:E + 16].indirect(T.lkl[:, 32 * j:32 * (j + n)]), F.Copy),
+           ["hit%d" % k, "hpad%d" % k, "lkl"], ["rem%d" % (j + d) for d in range(n)])
+
+    def sums(t, k, start, stop):
+        buf, c, key = (T.part, t, "part%d" % t) if k == r else (T.lanq, k, "lanq%d" % k) if t == last else (T.land, k, "land%d" % k)
+        for blk in range(4):
+            mm(col(T.m1, blk, 128), buf[:, c * E + 128 * blk:c * E + 128 * blk + 128], ident, start and blk == 0, stop and blk == 3, [key], "m1")
+
+    def d_pre():
+        mm(T.m1[:], n128i, T.eqv[:], True, False, ["id2", "eqv"], "m1")
+        mm(T.m1[:], n128i, T.none[:], False, False, ["id2", "none"], "m1")
+        sums(r, r, False, False)
+        for k in range(r):
+            mm(T.m1[:], col(T.dm, k, 128), col(T.rem, 2 * k + 1), False, False, ["dm", "rem%d" % (2 * k + 1)], "m1")
+
+    def x_pen():
+        terms = [(T.eqv, 0, n128i, "eqv"), (T.none, 0, n128i, "none")] + [
+            (T.rem, (2 * k + 1) * E, col(T.dm, k, 128), "rem%d" % (2 * k + 1)) for k in range(last - 1)]
+        for blk in range(4):
+            for n, (buf, c0, w, key) in enumerate(terms):
+                mm(col(T.m1, blk, 128), buf[:, c0 + 128 * blk:c0 + 128 * blk + 128], w, n == 0, n == len(terms) - 1, [key, "dm", "id2"], "m1")
+        op("ac", lambda: ac.activation(T.pen[:], T.m1[:], F.Copy), [], ["pen", "m1"])
+
+    def d_sum(t):
+        for k in others:
+            sums(t, k, False, k == others[-1])
+        op("ac", lambda: ac.activation(T.absa[:], T.m1[:], F.Abs, bias=float(16 * N)), [], ["absa", "m1"])
+
+    def d_ok(t):
+        op("ve", lambda: ve.tensor_scalar(T.ok[:], T.absa[:], 10.5, None, A.is_le), ["absa"], ["ok"])
+        mm(T.m1[:], T.gm[:], T.ok[:], True, True, ["gm", "ok"], "m1")
+        mm(T.m2[:], T.um[:], T.ok[:], True, True, ["um", "ok"], "m2")
+        op("ac", lambda: ac.activation(hit[t][:, 0:E], T.m1[:], F.Sign), [], ["hit%d" % t, "m1"])
+        if t < last:
+            bcast(hit[t][:], ["hpad%d" % t, "hit%d" % t], "arh%d" % t)
+
+    def d_first(t):
+        z, key = (col(T.zc, 2), "zc2") if t == last else (z16, zk)
+        op("ve", lambda: ve.tensor_scalar(T.first[:], T.m2[:], 0.0, None, A.max), [], ["first", "m2"])
+        op("ve", lambda: ve.tensor_tensor(T.mz[:], T.first[:], z, A.mult), ["first", key], ["mz"])
+        if t == r:
+            mm(T.m3[:], T.gm[:], T.mz[:], True, True, ["mz"], "m3")
+        mm(T.m2[:], T.gm[:], T.mz[:], True, False, ["mz"], "m2")
+        mm(T.m2[:], n1536i, hit[t][:, 0:E], False, True, ["id5", "hit%d" % t], "m2")
+
+    def d_sep(t):
+        c = int(t == last); sp = T.sep[0::16, c * E:(c + 1) * E]
+        op("ac", lambda: ac.activation(col(T.sep, c), T.m2[:], F.Identity, bias=float(V)), [], ["sep%d" % c, "m2"])
+        if t < last:
+            dmas("sy", "dsc", [(col(T.sepc, t, 32), sp, ["sep0"], ["sepc%d" % t])])
+        dmas("ac" if c else "sy", "do%d" % t, [(T.ysep[:, t * E:(t + 1) * E], sp, ["sep%d" % c], [])])
+
+    def d_send(t):
+        bcast(col(T.sepc, t, 32), ["sepc%d" % t], "ars%d" % t)
+
+    def d_eqs():
+        op("ve", lambda: ve.tensor_tensor(T.eqs[:], z16, T.m3[:], A.is_equal), [zk], ["eqs", "m3"])
+
+    def x_out(k):
+        if k != r:
+            dmas("sy", "do%d" % k, [(T.ysep[:, k * E:(k + 1) * E], col(T.sepc, k, 32), ["sepc%d" % k], [])])
+
+    def bc(i, bank, key, masked):
+        mm(bank, col(T.bm, i, 128), p16, True, not masked, ["bm", "p16"], key)
+        if masked:
+            mm(bank, p8ki, col(T.rem, 2 * i), False, True, ["id4", "rem%d" % (2 * i)], key)
+
+    def eq(i, bank, key):
+        op("ve", lambda: ve.tensor_tensor(col(T.eq, i), z16, bank, A.is_equal), [zk], ["eq%d" % i, key])
+
+    units = []; base = []
+    for t in range(RO):
+        sl = [i for i in range(16) if i != t]; base.append(len(units))
+        for u in UNITS[t].split():
+            units.append((t, sl[:int(u[1])], u[0])); sl = sl[int(u[1]):]
+    S = len(units)
+    extra = {}
+
+    def at(t, u, *fns):
+        extra.setdefault((base[t] if u >= 0 else (base + [S])[t + 1]) + u, []).extend(fns)
+
+    at(0, 1, x_rest); at(0, 2, x_z2); at(0, 4, x_lists); at(0, 5, lambda: x_scatter(0)); at(0, 7, lambda: x_scatter(1))
+    at(1, 0, x_p); at(1, 1, x_static); at(1, 2, x_eqv); at(1, 6, x_link); at(1, 8, x_linkl)
+    for t in range(1, RO):
+        for k, u in enumerate((-4, -2, -2, -1)):
+            at(t - 1, u, lambda t=t, k=k: prep(t, k))
+    for k in range(r):
+        if k + 2 <= last:
+            at(k + 2, 6 if k + 1 == r else 7 if k + 2 == last else 8, lambda k=k: x_rem(k, 1))
+    if r < last - 1:
+        at(r + 1, 7, d_pre, lambda: d_sum(r)); at(r + 1, 8, lambda: d_ok(r))
+        at(r + 2, 0, lambda: d_first(r), lambda: d_sep(r)); at(r + 2, 2, d_eqs); at(r + 2, 3, lambda: d_send(r))
+    elif r < last:
+        at(last, 7, d_pre, lambda: d_sum(r)); at(last, 8, lambda: d_ok(r)); at(last, 9, lambda: d_first(r), lambda: d_sep(r), d_eqs)
+    else:
+        at(last, 8, x_pen)
+    mb = [(T.m2[:], "m2"), (T.m3[:], "m3")]
+    todo = ([last] if r < last else []) + list(range(RO, 16)) + [i for i in range(last) if i != r]
+    for k in range(RO - 2):
+        at(k + 2, 6, lambda k=k: x_out(k))
+
+    DR = 4
+
+    def drain():
+        for n in range(DR - 2):
+            eq(todo[n], mb[n % 2][0], mb[n % 2][1]); bc(todo[n + 2], mb[n % 2][0], mb[n % 2][1], False)
+
+    extra.setdefault(S - 1, []).extend([lambda n=n: bc(todo[n], mb[n % 2][0], mb[n % 2][1], False) for n in (0, 1)])
+    extra.setdefault(S, []).append(drain)
+
+    def gat_v(s):
+        t, sl, kind = units[s]; c = t % 2; a = s % NA
+        for j, i in enumerate(sl):
+            op("ve", lambda: ve.tensor_tensor(col(T.ab, 2 * a + j), xw.indirect(lst(t, i)), col(T.lo, c), A.subtract),
+               ["xs", "xpad", "off%d_%d" % (t, i), "lo%d" % c], ["ab%d_%d" % (a, j)])
+        if kind == "v":
+            w = slice(1024 * a, 1024 * a + E * len(sl))
+            op("ve", lambda: ve.tensor_scalar(T.sa[:, w], T.ab[:, w], -1.0, 1.0, A.max, A.min),
+               ["ab%d_%d" % (a, j) for j in range(len(sl))], ["sa%d" % a])
+
+    def gat_s(s):
+        t, sl, kind = units[s]; a = s % NA
+        op("ac", lambda: ac.activation(col(T.ab, 2 * a), xw.indirect(lst(t, sl[0])), F.Copy),
+           ["xs", "xpad", "off%d_%d" % (t, sl[0])], ["ab%d_0" % a])
+
+    def pe_b(s):
+        t, sl, kind = units[s]; c = t % 2; a = s % NA; pb = T["pb%d" % (s % 2)]; kb = "pb%d_" % (s % 2)
+        if kind == "s":
+            for j in range(2):
+                mm(col(pb, j), nid, col(T.lo, c), True, False, ["id1", "lo%d" % c], kb + str(j))
+                if j == 0:
+                    mm(col(pb, j), ident, col(T.dl, c), False, False, ["dl%d" % c], kb + str(j))
+                mm(col(pb, j), ident, col(T.ab, 2 * a), False, True, ["id0", "ab%d_0" % a], kb + str(j))
+            return
+        for j in range(len(sl)):
+            mm(col(pb, j), ident, col(T.dl, c), True, False, ["id0", "dl%d" % c], kb + str(j))
+            mm(col(pb, j), ident, col(T.ab, 2 * a + j), False, True, ["ab%d_%d" % (a, j)], kb + str(j))
+
+    def sign_b(s):
+        t, sl, kind = units[s]; n = 2 if kind == "s" else len(sl); b = s % NS
+        op("ac", lambda: ac.activation(T.sb[:, 1024 * b:1024 * b + E * n], T["pb%d" % (s % 2)][:, 0:E * n], F.Sign),
+           [], ["sb%d" % b] + ["pb%d_%d" % (s % 2, j) for j in range(n)])
+
+    def sign_a(s):
+        t, sl, kind = units[s]; a = s % NA; w = slice(1024 * a, 1024 * a + E * len(sl))
+        op("ac", lambda: ac.activation(T.sa[:, w], T.ab[:, w], F.Sign), ["ab%d_%d" % (a, j) for j in range(len(sl))], ["sa%d" % a])
+
+    def pe_r(s):
+        t, sl, kind = units[s]; a = s % NA; b = s % NS
+        for j, i in enumerate(sl):
+            for blk in range(4):
+                o = T.red[:, 128 * blk + i:128 * blk + 128:16]; c0 = E * j + 128 * blk
+                if kind == "s":
+                    mm(o, T.sb[:, 1024 * b + E + c0:1024 * b + E + c0 + 128], T.ngm[:, 0::16], True, False, ["sb%d" % b, "ngm"], "red")
+                else:
+                    mm(o, T.sa[:, 1024 * a + c0:1024 * a + c0 + 128], T.ngm[:, 0::16], True, False, ["sa%d" % a, "ngm"], "red")
+                mm(o, T.sb[:, 1024 * b + c0:1024 * b + c0 + 128], T.gm[:, 0::16], False, True, ["sb%d" % b, "gm"], "red")
+
+    def evac(t):
+        op("ac", lambda: ac.activation(col(T.part, t), T.red[:], F.Copy), [], ["part%d" % t, "red"])
+        if t != r:
+            send_part(t)
+
+    for s in range(S + 1):
+        for fn in extra.get(s, []):
+            fn()
+        if s < S and units[s][2] != "s":
+            gat_v(s)
+        if s + 1 < S and units[s + 1][2] == "s":
+            gat_s(s + 1)
+        if s < S:
+            pe_b(s)
+        if s >= 1:
+            sign_b(s - 1)
+        if s >= 2 and s - 1 in base:
+            evac(units[s - 2][0])
+        if s < S and units[s][2] == "m":
+            sign_a(s)
+        if s >= 1:
+            pe_r(s - 1)
+
+    fb, fk = col(T.pb0, 0), "pb0_0"
+    banks = [(col(T.pb0, 1), "pb0_1"), (col(T.pb1, 0), "pb1_0"), (col(T.pb1, 1), "pb1_1")]
+    pos = [DR, DR]
+
+    def acc(i):
+        mm(fb, ident, col(T.eq, i), False, False, ["eq%d" % i], fk)
+
+    def ahead(n):
+        while pos[0] < min(n, len(todo)):
+            bc(todo[pos[0]], banks[pos[0] % 3][0], banks[pos[0] % 3][1], todo[pos[0]] < last); pos[0] += 1
+
+    def eqs(n):
+        for _ in range(n):
+            if pos[1] < len(todo):
+                ahead(pos[1] + 2)
+                eq(todo[pos[1]], banks[pos[1] % 3][0], banks[pos[1] % 3][1])
+                if pos[1] > DR:
+                    acc(todo[pos[1] - 1])
+                pos[1] += 1
+                if pos[1] == len(todo):
+                    acc(todo[-1])
+
+    def f_rem(k, stop):
+        mm(fb, col(T.dm, k, 128), col(T.rem, 2 * k + 1), False, stop, ["dm", "rem%d" % (2 * k + 1)], fk)
+
+    def f_own(stop):
+        mm(fb, p128i, hit[r][:, 0:E], False, False, ["id3", "hit%d" % r], fk)
+        mm(fb, n128i, T.eqs[:], False, stop, ["eqs"], fk)
+
+    for n in range(DR - 2, DR):
+        eq(todo[n], mb[n % 2][0], mb[n % 2][1])
+    if r == last:
+        op("ve", lambda: ve.tensor_tensor(col(T.part, last), T.red[:], T.pen[:], A.add), ["pen"], ["part%d" % last, "red"])
+    else:
+        op("ac", lambda: ac.activation(col(T.part, last), T.red[:], F.Copy), [], ["part%d" % last, "red"])
+    bcast(col(T.part, last), ["part%d" % last], "arq%d" % r, col(T.lanq, r))
+    if r == last - 1:
+        d_send(r)
+    for k in range(last - 1):
+        if k != r:
+            x_rem(k, 0, 2 if k > r else 1)
+    rm4, rmk = col(T.rem, 2 * last - 1), "rem%d" % (2 * last - 1)
+    if r < last:
+        rm4, rmk = T.rm4[:], "rm4"
+        op("ac", lambda: ac.activation(rm4, hit[last - 1][:, 0:E + 16].indirect(T.lk4[:]), F.Copy),
+           ["hit%d" % (last - 1), "hpad%d" % (last - 1), "lk4"], [rmk])
+    if r != last - 1:
+        x_rem(last - 1, 0, 2)
+    ahead(DR + 2)
+    mm(fb, n128i, T.none[:], True, False, ["none"], fk)
+    for i in todo[:DR]:
+        if i != last:
+            acc(i)
+    if r < last:
+        f_own(False)
+    x_out(last - 1)
+    eqs(TAIL[0])
+    mm(T.m1[:], col(T.dm, last - 1, 128), rm4, True, False, ["dm", rmk], "m1")
+    sums(last, r, False, False)
+    d_sum(last); eqs(TAIL[1]); d_ok(last); eqs(TAIL[2])
+    for k in range(last):
+        if k != r:
+            f_rem(k, False)
+    if r < last:
+        x_rem(last, 1)
+        eqs(16)
+        op("ve", lambda: ve.tensor_tensor(col(T.eq, 16), hit[last][:, 0:E + 16].indirect(col(T.lkl, 2 * last, 32)), col(T.eq, last), A.is_lt),
+           ["hit%d" % last, "hpad%d" % last, "lkl", "eq%d" % last], ["eq16"])
+        acc(16); f_rem(last, True)
+        d_first(last)
+    else:
+        d_first(last); eqs(16); d_eqs(); f_own(True)
+    op("ve", lambda: ve.tensor_scalar(T.flag[:], fb, 128.5, None, A.is_gt), [], ["flag", fk])
+    d_sep(last)
+    dmas("sy", "dfl", [(T.yflag[:], T.flag[:], ["flag"], [])])
+    for s in cnt:
+        need("po", (s, cnt[s]))

@@ -2,523 +2,525 @@ from concourse.bass import DstId, RemoteDMATransfer
 from concourse.mybir import AluOpType as A, ActivationFunctionType as F
 
 V, E, RO, N = 3072, 512, 5, 5
+LAST = RO - 1
 LW = 18 * 32
 OFS = 1536
-NA, NS = 4, 3
-UNITS = ["v2 s1 v2 s1 m2 s1 m2 s1 v2 s1",
-         "v2 v2 s1 v2 s1 m2 s1 v2 v2",
-         "v2 v2 s1 v2 s1 m2 s1 v2 v2",
-         "v2 v2 s1 v2 s1 m2 s1 v2 v2",
-         "v2 s1 v2 s1 v2 s1 v2 v2 v1 v1"]
-TAIL = (9, 1, 1)
+BIG = 1.5 * 2 ** 28
+NA, NG = 4, 3
+UNITS = ["s1 v2 m2 s1 v2 v2 s1 v2 v2"] * 2 + ["s1 v2 m2 v2 s1 v2 m2 v2 v1"] * 2 + ["s1 v2 v2 v2 v2 v2 v2 v2"]
+EARLY = [0, 4, 4, 4, 2]
+EQ4 = 6
+PREP = 5
+FREE_V, FREE_A = 1, 6
+M3, REDP, DLAT, GPR = 8, 1.3, 3000, 1
+CY, PC, GA, SC, HOP, SLACK, URGENT, MARGIN = 0.9, 0.44, 1.5, 3.5, 120, 100, 150, 2000
+LATE = (6000, 3500, 2000, 500, 2500, 1500, 1000, 300)
 BF, F16, F32 = "bfloat16", "float16", "float32"
-SB = {"adjs": (V, "int32"), "adj0": (V, "int32"), "xs": (V + 16, BF), "tvs": (160, "int32"),
-      "ti": (V, F32), "tic": (5 * 192, F32), "io2": (E, F32), "onesb": (2048, BF), "n128": (640, BF),
-      "sw": (512, BF), "idm": (6 * 128, BF), "g0": (128, BF), "gm": (128, BF), "ngm": (128, BF), "u0": (128, BF), "um": (128, BF),
-      "dm": (640, BF), "bm": (2048, BF), "pc": (1024, F16), "pt": (1024, F16), "zc": (3 * E, F16), "zt": (1024, F16),
-      "off": (5 * LW, "uint16"), "none": (E, BF), "eqv": (E, BF), "pen": (E, BF), "lk": (1024, F16), "lt": (1024, F16),
-      "lkl": (320, "uint16"), "rem": (10 * E, BF), "lk4": (32, "uint16"), "rm4": (E, BF),
-      "xy": (2 * E, BF), "dd": (2 * E, BF), "ad": (2 * E, BF), "lo": (2 * E, BF), "dl": (2 * E, BF),
-      "ab": (NA * 1024, BF), "sa": (NA * 1024, BF), "sb": (NS * 1024, BF), "part": (5 * E, BF), "land": (5 * E, BF), "lanq": (5 * E, BF),
-      "absa": (E, BF), "ok": (E, BF), "first": (E, BF), "mz": (E, F16), "sep": (2 * E, F32), "sepc": (5 * 32, F32),
-      "eqs": (E, BF), "eq": (17 * E, BF), "flag": (E, BF),
-      "hit0": (E + 16, BF), "hit1": (E + 16, BF), "hit2": (E + 16, BF), "hit3": (E + 16, BF), "hit4": (E + 16, BF)}
+SB = {"adjs": (V, "int32"), "adj0": (V, "int32"), "xs": (V + 16, BF), "tvs": (160, "int32"), "vl": (160, "uint16"),
+      "ti": (V, F32), "tic": (5 * 192, F32), "io2": (E, F32), "onesb": (OFS, BF), "n256": (E, BF), "sw": (E, BF),
+      "idm": (9 * 128, BF), "gm": (9 * 128, BF), "cm": (256, BF), "dm": (E, BF), "bm": (2048, BF),
+      "py": (E, F16), "pc": (E, F16), "pt": (E, F16), "zc": (2 * E, F16), "zt": (E, F16), "zall": (16 * E, F16),
+      "off": (5 * LW, "uint16"), "none": (E, BF), "eqv": (E, BF), "lk": (1024, F16), "lt": (1024, F16),
+      "lkl": (320, "uint16"), "rem": (8 * E, BF), "lk4": (32, "uint16"), "rm4": (E, BF),
+      "xv": (5 * E, BF), "xy": (2 * E, BF), "ad": (E, BF), "lo": (10 * E, BF), "dl": (10 * E, BF),
+      "ab": ((NA + NG) * 1024, BF), "sa": ((NA + NG) * 1024, BF), "sb": ((NA + NG) * 1024, BF),
+      "part": (6 * E, BF), "land": (5 * E, BF), "lanq": (5 * E, BF), "ok": (E, BF), "mz": (E, F16),
+      "sep": (2 * E, F32), "sepc": (5 * 32, F32), "eqs": (E, BF), "eq": (16 * E, BF), "fp": (2 * E, BF), "flag": (E, BF)}
+SB.update({"hit%d" % k: (E + 16, BF) for k in range(6)})
 SCRATCH = {k: ("sbuf", [128, w], d) for k, (w, d) in SB.items()}
-SCRATCH.update({k: ("psum", [128, w], F32) for k, w in (("pb0", 1024), ("pb1", 1024), ("red", E), ("m1", E), ("m2", E), ("m3", E))})
-SEMAPHORES = (["ve", "ac", "pe", "po", "ls", "arp", "arz", "ark", "dtv", "dadj", "dadj0", "dx", "dtc", "dtr", "dsc", "dfl"]
-              + ["do%d" % k for k in range(5)] + ["ar%s%d" % (a, k) for a in "lthsq" for k in range(5)])
+SCRATCH.update({k: ("psum", [128, w], F32) for k, w in (("pb0", 1024), ("pb1", 1024), ("pb2", 1024), ("red", E), ("m1", E))})
+SEMAPHORES = (["ve", "ac", "pe", "po", "ls", "arp", "arz", "ark", "arw6", "arw12", "dtv", "dadj", "dadj0", "dx", "dtc", "dtr", "dsc", "dfl"]
+              + ["%s%d" % (a, k) for a in ("do", "dd", "de", "dz", "ary", "arl", "art", "arh", "ars", "arq") for k in range(5)]
+              + ["da%d" % k for k in range(NA + NG)])
+PLAN = []
+
+
+def build(r, g, T, topo):
+    core = T.cores[r]; ops = []
+    ve, ac, pe = g.vector, g.scalar, g.tensor
+    others = [k for k in range(N) if k != r]
+
+    def add(q, fns, R, W, cost, pr=1, lat=0, sem=None, sends=()):
+        ops.append(dict(q=q, fns=fns, R=list(R), W=list(W), cost=cost, pr=pr, lat=lat, sem=sem, sends=sends, r=r))
+
+    def vop(fn, R, W, n, pr=1):
+        add("ve", [fn], R, W, 50 + max(64, n) * CY, pr)
+
+    def aop(fn, R, W, n, pr=1):
+        add("ac", [fn], R, W, 65 + max(64, n) * CY, pr)
+
+    def pop(fn, R, W, n, pr=1):
+        add("po", [fn], R, W, 170 + 2 * n * CY, pr)
+
+    def mms(items, R, W, pr=1):
+        add("pe", [lambda m=m: pe.matmul(*m) for m in items], R, W, sum(PC * max(64, m[2].shape[1]) for m in items), pr)
+
+    def mm(out, lhsT, rhs, start, stop, R, bank, pr=1):
+        mms([(out, lhsT, rhs, start, stop)], R, [bank], pr)
+
+    def dma(q, sem, items, R, W, lat=2000, pr=0):
+        Q = g.sync if q == "sy" else ac
+        add(q, [lambda m=m: Q.dma_start(*m) for m in items], R, W, 60 * len(items), pr, lat, sem)
+
+    def dst(k):
+        rid, pid, se = topo.addr(T.cores[k])
+        return DstId(rid=rid, pnc=pid)
+
+    def bcast(ap, keys, sem, nbytes, to=None, tkeys=None, margin=MARGIN, ranks=others):
+        el = [topo.engines(core, T.cores[k])[n::1 if len(ranks) == 1 else len(others)] for n, k in enumerate(ranks)]
+        tr = [RemoteDMATransfer(dst_ids=[dst(k)], dma_engine_mask=sum(1 << e for e in el[n]), remote_sem=T.sem[sem], src=ap,
+                                dst=ap if to is None else to) for n, k in enumerate(ranks)]
+        add("po", [lambda: g.remote_dma_fused(tr, local_sem=T.sem.ls)], keys, [], 700, 0, 1600 + 1.5 * nbytes + margin, "ls",
+            [(k, tkeys or keys[:16], sem, len(el[n])) for n, k in enumerate(ranks)])
+
+    col = lambda buf, k, w=E: buf[:, k * w:(k + 1) * w]
+    lst = lambda t, i, n=1: T.off[:, t * LW + 32 * i:t * LW + 32 * (i + n)]
+    lk_ = lambda t, i, n=1: ["off%d_%d" % (t, j) for j in range(i, i + n)]
+    xw, aw, ob = T.xs[:, 0:V + 16], T.adjs[:, 0:V], T.onesb[:, 0:128]
+    ident, nid, i15, n256i, p128i, p32i, p2i, nsi, md = [col(T.idm, k, 128) for k in range(9)]
+    g0, gm, ngm, um, wm, gm4, w0, u0, w1 = [col(T.gm, k, 128) for k in range(9)]
+    hit = [T["hit%d" % k] for k in range(6)]
+    z16, p16, zk = col(T.zc, int(r == LAST)), T.pc[:], "zc%d" % int(r == LAST)
+    G1 = GA * E; XS = ["xs", "xpad"]
+
+    dma("ac", "dtv", [(T.tvs[:], T.tv[:])], [], ["tvs"], 1800)
+    dma("sy", "dx", [(T.xs[:, 0:V], T.x[:])], [], ["xs"], 3600)
+    vop(lambda: ve.memset(ob, 1.0), [], ["ob"], 64)
+    vop(lambda: ve.memset(T.onesb[:, 128:OFS], 1.0), [], ["onesb"], 704)
+    vop(lambda: ve.memset(T.adj0[:, 0:2048], 0), [], ["adja"], 2048)
+    pop(lambda: g.iota(T.adj0[:, 2048:V], [[0, 1024]], 0, 0), [], ["adjb"], 1024)
+    dma("sy", "dadj0", [(T.adj0[r::16, :], T.adj[r::16, :])], ["adja", "adjb"], ["adj0"], 1800)
+    dma("sy", "dadj", [(T.adjs[:], T.adj[:])], ["adja", "adjb"], ["adjs"], 6200)
+
+    def const(out, src, R, key, scale):
+        aop(lambda: ac.activation(out, src, F.Identity, scale=float(scale)), R, [key], out.shape[1])
+
+    for h in range(2):
+        const(col(T.ti, h, OFS), T.onesb[:], ["ob", "onesb"], "ti", E)
+    pop(lambda: g.iota(T.io2[:], [[1, E]], 0, 0, allow_small_or_imprecise_dtypes=True), [], ["io2"], E)
+    for n in range(4):
+        pop(lambda n=n: g.affine_select(col(T.sw, n, 128), ob, [[-32, 4], [128, 2], [-1, 16]], A.is_equal, 0.0, -16 * (n // 2) - 128 * (n % 2), 1),
+            ["ob"], ["sw%d" % n], 128)
+    pop(lambda: g.affine_select(ident, ob, [[-1, 128]], A.is_equal, 0.0, 0, 1), ["ob"], ["id0"], 128)
+
+    def ingroup(out, src, key, okey):
+        pop(lambda: g.affine_select(g0, src, [[-16, 8], [0, 16]], A.is_ge, 0.0, 0, 1), [key], ["g0"], 128)
+        pop(lambda: g.affine_select(out, g0, [[16, 8], [0, 16]], A.is_ge, 0.0, 15, -1), ["g0"], [okey], 128)
+
+    ingroup(gm, ob, "ob", "gm")
+    vop(lambda: ve.tensor_copy(T.vl[:], T.tvs[:]), ["tvs"], ["vl"], 160, 0)
+    vop(lambda: ve.tensor_copy(lst(r, 17), T.tvs[:, 32 * r:32 * r + 32]), ["tvs"], lk_(r, 17), 64, 0)
+    vop(lambda: ve.memset(T.xs[:, V:V + 16], 300.0), [], ["xpad"], 64)
+    vop(lambda: ve.memset(T.n256[:], -256.0), [], ["n256"], 256)
+    vop(lambda: ve.memset(T.red[:], 0.0), [], ["red"], E)
+    vop(lambda: ve.memset(T.cm[:, 0:128], -12.0), [], ["cm0"], 64)
+    vop(lambda: ve.memset(T.cm[:, 128:256], 204.0), [], ["cm1"], 64)
+    for k in sorted({r, LAST, 5}):
+        vop(lambda k=k: ve.memset(hit[k][:, E:E + 16], 0.0), [], ["hpad%d" % k], 64)
+
+    def scatter(h):
+        vop(lambda: ve.tensor_copy(T.ti[:, 0:V].indirect(lst(r, 16 + h)), T.io2[:]), ["io2"] + lk_(r, 16 + h), ["ti"], SC * E)
+
+    scatter(1)
+    for t0, n in ((r, 1), (0, r), (r + 1, LAST - r)):
+        if n:
+            aop(lambda t0=t0, n=n: ac.activation(T.xv[:, t0 * E:(t0 + n) * E], xw.indirect(T.vl[:, 32 * t0:32 * (t0 + n)]), F.Copy),
+                XS + ["vl"], ["xv%d" % t for t in range(t0, t0 + n)], n * G1, 0 if t0 == r else 1)
+    for k, c in enumerate((-1, 1.5, -256, 128, 32, 2, -1 / 256)):
+        const(col(T.idm, k + 1, 128), ident, ["id0"], "id%d" % (k + 1), c)
+    const(ngm, gm, ["gm"], "ngm", -1)
+    const(u0, gm, ["gm"], "u0", -2 * OFS)
+    for c in ((0,), (1, 2))[r == LAST]:
+        pop(lambda c=c: g.affine_select(col(T.bm, c), T.onesb[:, 0:E], [[-1, 4], [-16, 8], [0, 16]], A.is_equal, 0.0, -4 * c, 1),
+            ["ob", "onesb"], ["bm%d" % c], E)
+
+    def rows(dstb, i, key, win=aw, wk="adjs", pr=0):
+        vop(lambda: ve.tensor_scalar(dstb, win.indirect(lst(r, i)), -float(OFS), None, A.add), [wk] + lk_(r, i), [key], G1, pr)
+
+    def swap(bank, c0, src, i, n, key, bkey):
+        mms([(bank[:, c0 + q:c0 + 2 * n:2], col(T.sw, 2 * q + gl, 128), src[:, 16 * gl + i::32], gl == 0, gl == 1) for q in range(2) for gl in range(2)],
+            ["sw0", "sw1", "sw2", "sw3", key], [bkey], 0)
+
+    def turn(dstb, src, key, dkey, n=E):
+        vop(lambda: ve.transpose(dstb, src), [key], [dkey], n // 2, 0)
+
+    def tolist(i, n, bank, bkey):
+        vop(lambda: ve.tensor_scalar(lst(r, i, n), bank, float(OFS), None, A.add), [], lk_(r, i, n) + [bkey], 32 * n, 0)
+
+    rows(T.py[:], 17, "py", T.adj0[:, 0:V], "adj0"); turn(T.pt[:], T.py[:], "py", "pt"); swap(T.m1, 0, T.pt, r, 16, "pt", "m1")
+    tolist(16, 1, T.m1[:, 0:32], "m1")
+    bcast(lst(r, 16), lk_(r, 16), "ary%d" % r, 64, margin=0)
+    rows(z16, 16, zk); turn(T.zt[:], z16, zk, "zt")
+    for i0, n, bank, key in ((12, 4, T.m1, "m1"), (6, 6, T.pb1, "pb1_0"), (0, 6, T.m1, "m1")):
+        for i in range(i0, i0 + n):
+            swap(bank, 32 * i, T.zt, i, 16, "zt", key)
+        tolist(i0, n, bank[:, 32 * i0:32 * (i0 + n)], key)
+        if r == 0:
+            bcast(lst(0, i0, n), lk_(0, i0, n), "arl0" if i0 == 0 else "arw%d" % i0, 64 * n, margin=2500)
+    if r:
+        bcast(lst(r, 0, 16), lk_(r, 0, 16), "arl%d" % r, 1024)
+    if r == LAST:
+        bcast(z16, [zk], "arz", 1024)
+    pop(lambda: g.affine_select(um, u0, [[1, 128]], A.is_gt, 0.0, 0, -1), ["u0"], ["um"], 128)
+    pop(lambda: g.affine_select(um, um, [[-1, 128]], A.not_equal, 2.0 * OFS, 0, 1), [], ["um"], 128)
+    pop(lambda: g.affine_select(T.dm[:], T.n256[:], [[-128, 4], [-16, 8], [128, 16]], A.is_equal, 0.0, 0, 1), ["n256"], ["dm"], E)
+    pop(lambda: g.iota(w0, [[-16, 8], [0, 16]], -14, 1, allow_small_or_imprecise_dtypes=True), [], ["w0"], 128)
+    ingroup(w0, w0, "w0", "w0")
+    pop(lambda: g.affine_select(gm4, gm, [[0, 8], [1, 16]], A.is_equal, 0.0, -LAST, 0), ["gm"], ["gm4"], 128)
+
+    seen = {"a": 0, "p": 0, "s": 0}
+
+    def take(key):
+        seen[key] += 1
+        return seen[key] - 1
+
+    def ring(side=False):
+        p = 2 if side else take("p") % 2
+        return T["pb%d" % p], ["pb%d_0" % p, "pb%d_1" % p]
+
+    def prep(t):
+        xv, xy, kv, ky = col(T.xv, t), col(T.xy, t % 2), "xv%d" % t, "xy%d" % (t % 2)
+        aop(lambda: ac.activation(xy, xw.indirect(lst(t, 16)), F.Copy), XS + lk_(t, 16), [ky], G1, 1 if t and t != r else 0)
+        pb, kb = ring(True); lo = col(T.lo, 2 * t)
+        mm(col(pb, 0), ident, xv, True, True, ["id0", kv], kb[0], -1)
+        mms([(col(pb, 1), ident, xv, True, False), (col(pb, 1), nid, xy, False, True)], ["id1", kv, ky], [kb[1]], -1)
+        vop(lambda: ve.tensor_tensor(lo, xy, col(pb, 0), A.min), [ky], ["lo%d" % t, kb[0]], E, -1)
+        aop(lambda: ac.activation(T.ad[:], col(pb, 1), F.Abs), [], ["ad", kb[1]], E, -1)
+        vop(lambda: ve.tensor_scalar(col(T.dl, 2 * t), T.ad[:], 0.5, -1.0, A.max, A.mult), ["ad"], ["dl%d" % t], E // 2, -1)
+        for kind, buf, key in (("d", T.dl, "dl"), ("e", T.lo, "lo")):
+            if kind in UNITS[t]:
+                dma("sy", "d%s%d" % (kind, t), [(col(buf, 2 * t + 1), col(buf, 2 * t))], ["%s%d" % (key, t)], ["%s2%d" % (key, t)])
+
+    prep(r)
+
+    def links():
+        scatter(0)
+        dma("sy", "dtc", [(col(T.tic, r, 192), T.ti[r::16, :])], ["ti"], ["tic%d" % r])
+        add("po", [], lk_(r, 0) + ["tic%d" % r], ["tic%d" % r], 0, 0)
+        bcast(col(T.tic, r, 192), ["tic%d" % r], "art%d" % r, 768)
+        dma("sy", "dtr", [(T.ti[k::16, :], col(T.tic, k, 192)) for k in others], ["tic%d" % k for k in others], ["ti"], 3000)
+        rows(p16, 17, "p16", pr=1)
+        vop(lambda: ve.tensor_scalar(wm, w0, -2.0 * OFS, None, A.mult), ["w0"], ["wm"], 64)
+        vop(lambda: ve.tensor_scalar(T.none[:], z16, V - OFS - 0.5, None, A.is_ge), [zk], ["none"], 256)
+        mm(T.m1[:], col(T.bm, r, 128), z16, True, True, ["bm%d" % (r // 4), zk], "m1")
+        vop(lambda: ve.tensor_tensor(T.eqv[:], z16, T.m1[:], A.is_equal), [zk], ["eqv", "m1"], E)
+        vop(lambda: ve.tensor_copy(T.lk[:], T.ti[:, 0:V].indirect(lst(r, 16, 2))), ["ti"] + lk_(r, 16, 2), ["lk"], 2 * G1, 0)
+        turn(T.lt[:], T.lk[:], "lk", "lt", 1024)
+        for k in range(RO):
+            swap(T.m1, 64 * k, T.lt, k, 32, "lt", "m1")
+        vop(lambda: ve.tensor_copy(T.lkl[:], T.m1[:, 0:320]), [], ["lkl", "m1"], 320, 0)
+        if r == LAST:
+            bcast(col(T.lkl, 2 * LAST - 2, 32), ["lkl"], "ark", 64, T.lk4[:], ["lk4"])
+        const(w1, col(T.bm, r, 128), ["bm%d" % (r // 4)], "w1", 1 / 256)
+        vop(lambda: ve.tensor_tensor(md, w1, nsi, A.add), ["w1", "id7"], ["md"], 256)
+
+    def copies():
+        dma("sy", "dz0", [(col(T.zall, n), z16) for n in range(4)], [zk, "quiet"], ["zall"], 4000, 1)
+        dma("sy", "dz1", [(col(T.zall, n, 4 * E), col(T.zall, 0, 4 * E)) for n in range(1, 4)], [], ["zall"], 6000, 1)
+        dma("sy", "dz2", [(T.zall[r::16, :], p16)], ["p16"], ["zall"], 2500, 1)
+
+    def rem(k, side, n=1, pr=0, R=()):
+        j = 2 * k + side
+        aop(lambda: ac.activation(T.rem[:, j * E:(j + n) * E], hit[k][:, 0:E + 16].indirect(T.lkl[:, 32 * j:32 * (j + n)]), F.Copy),
+            ["hit%d" % k, "hpad%d" % k, "lkl"] + list(R), ["rem%d" % (j + d) for d in range(n)], n * G1, pr)
+
+    def turned(bank, key, buf, c, w, R, start=False, stop=False):
+        mms([(col(bank, b, 128), buf[:, c * E + 128 * b:c * E + 128 * b + 128], w, start and b == 0, stop and b == 3) for b in range(4)], R, [key], 0)
+
+    def decide(t, ub, uk, bb, bk):
+        z, key = (col(T.zc, 1), "zc1") if t == LAST else (z16, zk)
+        for k in others:
+            buf, kk = (T.lanq, "lanq%d" % k) if t == LAST else (T.land, "land%d" % k)
+            turned(T.m1, "m1", buf, k, i15, [kk], False, k == others[-1])
+        vop(lambda: ve.tensor_scalar(T.ok[:], T.m1[:], BIG, BIG, A.add, A.is_equal), [], ["ok", "m1"], E, 0)
+        mm(T.m1[:], gm, T.ok[:], True, True, ["gm", "ok"], "m1", 0)
+        if t == LAST and r < LAST:
+            mm(col(T.pb1, 0), gm4, T.ok[:], True, True, ["gm4", "ok"], "pb1_0", 0)
+        aop(lambda: ac.activation(hit[t][:, 0:E], T.m1[:], F.Sign), [], ["hit%d" % t, "m1"], E, 0)
+        if t < LAST:
+            for to in ([t + 1], [k for k in others if k != t + 1]) if t < LAST - 1 else (others,):
+                bcast(hit[t][:], ["hpad%d" % t, "hit%d" % t], "arh%d" % t, 264 if len(to) == 1 else 1056,
+                      margin=LATE[4 + t] + (3000 if len(to) == 3 else 0), ranks=to)
+        elif r < LAST:
+            aop(lambda: ac.activation(hit[5][:, 0:E], col(T.pb1, 0), F.Sign), [], ["hit5", "pb1_0"], E, 0)
+            vop(lambda: ve.tensor_tensor(col(T.fp, 1), hit[LAST][:, 0:E + 16].indirect(col(T.lkl, 2 * LAST + 1, 32)), col(T.fp, 0), A.is_lt),
+                ["hit%d" % LAST, "hpad%d" % LAST, "lkl", "fp0"], ["fp1"], G1, 0)
+            vop(lambda: ve.tensor_tensor(T.flag[:], hit[5][:, 0:E + 16].indirect(col(T.lkl, 2 * LAST, 32)), col(T.fp, 1), A.is_lt),
+                ["hit5", "hpad5", "lkl", "fp1"], ["flag"], G1, 0)
+        mm(ub, T.cm[:, 0:128], T.onesb[:, 0:E], True, False, ["cm0", "ob", "onesb"], uk, 0)
+        mm(ub, um, T.ok[:], False, True, ["um", "ok"], uk, 0)
+        vop(lambda: ve.tensor_tensor(T.mz[:], z, ub, A.min), [key], ["mz", uk], E, 0)
+        mm(bb, T.cm[:, 128:256], T.onesb[:, 0:E], True, False, ["cm1", "ob", "onesb"], bk, 0)
+        mm(bb, wm, T.ok[:], False, False, ["wm", "ok"], bk, 0)
+        mm(bb, gm, T.mz[:], False, True, ["mz"], bk, 0)
+        c = int(t == LAST); sp = T.sep[0::16, c * E:(c + 1) * E]
+        if t == r == LAST:
+            vop(lambda: ve.tensor_tensor(T.eqs[:], z16, bb, A.is_equal), [zk], ["eqs", bk], E, 0)
+        aop(lambda: ac.activation(col(T.sep, c), bb, F.Identity, bias=float(OFS)), [], ["sep%d" % c, bk], E, 0)
+        if t < LAST:
+            vop(lambda: ve.tensor_tensor(T.eqs[:], z16, bb, A.is_equal), [zk], ["eqs", bk], E, 0)
+            dma("sy", "dsc", [(col(T.sepc, t, 32), sp)], ["sep0"], ["sepc%d" % t])
+            bcast(col(T.sepc, t, 32), ["sepc%d" % t], "ars%d" % t, 128)
+        dma("ac" if c else "sy", "do%d" % t, [(T.ysep[:, t * E:(t + 1) * E], sp)], ["sep%d" % c], [])
+
+    def own():
+        mm(T.m1[:], n256i, T.eqv[:], True, False, ["id3", "eqv"], "m1", 0)
+        turned(T.m1, "m1", T.part, r, i15, ["id2", "part%d" % r])
+        for k in range(r):
+            rem(k, 0)
+            mm(T.m1[:], col(T.dm, k, 128), col(T.rem, 2 * k), False, False, ["dm", "rem%d" % (2 * k)], "m1", 0)
+        decide(r, T.m1[:], "m1", T.m1[:], "m1")
+
+    rounds = []
+    for t in range(RO):
+        sv = [i for i in range(16) if i != t]; un = []
+        for u in UNITS[t].split():
+            n = int(u[1]); un.append((t, sv[-n:], u[0])); sv = sv[:-n]
+        rounds.append(un)
+    e0 = EARLY[r]
+    units = rounds[r][:e0] + [u for t in range(RO) for u in (rounds[t][e0:] if t == r else rounds[t])]
+    S = len(units)
+
+    def unit(s):
+        t, sl, kind = units[s]; n = len(sl)
+        a = NA + take("s") % NG if kind in "se" else take("a") % NA
+        ab, sa, sb = [buf[:, 1024 * a:1024 * a + E * n] for buf in (T.ab, T.sa, T.sb)]
+        ka, ksa, ksb = [["%s%d_%d" % (x, a, j) for j in range(n)] for x in ("ab", "sa", "sb")]
+        lo, dl = col(T.lo, 2 * t), col(T.dl, 2 * t)
+        rv = ["relv"] if s == S - FREE_V else []; ra = ["rela"] if s == S - FREE_A else []
+        if s > e0 + 2 and units[s - 2][0] == int(r == 0) != units[s - 1][0]:
+            ra = ra + ["quiet"]
+        tiles = [(col(sa, j), col(sb, j)) for j in range(n)]
+        if kind in "se":
+            aop(lambda: ac.activation(ab, xw.indirect(lst(t, sl[0], n)), F.Copy, scale=1.0 if kind == "s" else -1.0), XS + lk_(t, sl[0], n), ka, n * G1, GPR)
+        else:
+            for j, i in enumerate(sl):
+                vop(lambda j=j, i=i: ve.tensor_tensor(col(ab, j), xw.indirect(lst(t, i)), lo, A.subtract), XS + ["lo%d" % t] + lk_(t, i), [ka[j]], G1)
+        if kind == "s":
+            for j in range(n):
+                pb, kb = ring(True); out = col((T.sa, T.sb)[j], a, 1024); tiles[j] = (col(out, 0), col(out, 1))
+                mms([(col(pb, h), nid, lo, True, False) for h in range(2)] + [(col(pb, 1), ident, dl, False, False)], ["id1", "lo%d" % t, "dl%d" % t], kb)
+                mms([(col(pb, h), ident, col(ab, j), False, True) for h in range(2)], ["id0", ka[j]], kb)
+                aop(lambda out=out, pb=pb: ac.activation(out, pb[:], F.Sign), [], [ksa[j], ksb[j]] + kb + ra, 2 * E)
+        else:
+            if kind == "e":
+                add("po", [lambda: g.dma_start(ab, T.lo[:, 1024 * t:1024 * t + E * n], accum_op=A.add)], ["lo%d" % t, "lo2%d" % t], ka, 1000, 0, DLAT, "da%d" % a)
+            if kind == "m":
+                aop(lambda: ac.activation(sa, ab, F.Sign), ka, ksa + rv, n * E)
+            else:
+                vop(lambda: ve.tensor_scalar(sa, ab, -1.0, 1.0, A.max, A.min), ka, ksa + rv, n * 256)
+            if kind == "d":
+                add("po", [lambda: g.dma_start(ab, T.dl[:, 1024 * t:1024 * t + E * n], accum_op=A.add)], ["dl%d" % t, "dl2%d" % t], ka, 1000, 0, DLAT, "da%d" % a)
+                aop(lambda: ac.activation(sb, ab, F.Sign), ka, ksb + ra, n * E)
+            else:
+                pb, kb = ring(kind == "e")
+                for j in range(n):
+                    mm(col(pb, j), nid if kind == "e" else ident, dl, True, False, ["id0", "id1", "dl%d" % t], kb[j])
+                    mm(col(pb, j), ident, col(ab, j), False, True, [ka[j]], kb[j])
+                aop(lambda: ac.activation(sb, pb[:, 0:E * n], F.Sign), [], ksb + kb[:n] + ra, n * E)
+        wa, wb = (gm, ngm) if kind == "e" else (ngm, gm)
+        one = t == r and r and s >= e0
+        fin = s + 1 == S or units[s + 1][0] != t or s + 1 == e0
+        if one and (s == e0 or units[s - 1][0] != t):
+            mm(T.red[:], ident, col(T.part, 5), True, False, ["part5"], "red")
+        if one and fin and r == LAST:
+            turned(T.red, "red", T.eqv, 0, n256i, ["eqv", "id3"])
+            for k in range(LAST - 1):
+                rem(k, 0)
+                turned(T.red, "red", T.rem, 2 * k, col(T.dm, k, 128), ["dm", "rem%d" % (2 * k)])
+        it = []
+        for j, i in enumerate(sl):
+            for blk in range(4):
+                o = T.red[:, 128 * blk + i:128 * blk + 128:16]
+                it += [(o, col(tiles[j][0], blk, 128), wa[:, 0::16], not one, False),
+                       (o, col(tiles[j][1], blk, 128), wb[:, 0::16], False, not one or (fin and j == n - 1 and blk == 3))]
+        if one and fin:
+            mms(it, ksa + ksb + ["gm", "ngm"], ["red"])
+        else:
+            mms(it, ksa + ksb + ["gm", "ngm", "red"], [], REDP)
+        if fin:
+            c = 5 if s < e0 else t
+            aop(lambda: ac.activation(col(T.part, c), T.red[:], F.Identity, bias=16.0 * (c < 5)), [], ["part%d" % c, "red"], E, 0)
+            if c == LAST:
+                bcast(col(T.part, LAST), ["part%d" % LAST], "arq%d" % r, 1024, col(T.lanq, r), ["lanq%d" % r], 0)
+            elif c == r:
+                own()
+            elif c < LAST:
+                bcast(col(T.part, t), ["part%d" % t], "arp", 0, col(T.land, r), ["land%d" % r], LATE[t], [t])
+
+    ahead = EQ4 if r == LAST else 0
+    made = {r}
+    for s in range(S):
+        t = units[min(s + PREP, S - 1)][0]
+        if t not in made and (s >= 1 or not r):
+            made.add(t); prep(t)
+        if s == 0:
+            links()
+        if s == 1:
+            for i in range(RO, RO + ahead):
+                bank, key = col(T.pb1, i % 2), "pb1_%d" % (i % 2)
+                mm(bank, col(T.bm, i, 128), p16, True, True, ["bm%d" % (i // 4), "p16"], key)
+                vop(lambda i=i, bank=bank: ve.tensor_tensor(col(T.eq, i), z16, bank, A.is_equal), [zk], ["eq%d" % i, key], E)
+        unit(s)
+    copies()
+
+    fb, fk = col(T.pb0, 0), "pb0_0"
+    banks = [(col(T.pb2, 0), "pb2_0"), (col(T.pb2, 1), "pb2_1"), (col(T.pb1, 1), "pb1_1")]
+    for k in range(LAST):
+        if k != r:
+            both = k > r or k == LAST - 1
+            rem(k, 0 if both else 1, 2 if both else 1, 2, ["rela"])
+    rm4, rmk = col(T.rem, 2 * LAST - 2), "rem%d" % (2 * LAST - 2)
+    if r < LAST:
+        rm4, rmk = T.rm4[:], "rm4"
+        aop(lambda: ac.activation(rm4, hit[LAST - 1][:, 0:E + 16].indirect(T.lk4[:]), F.Copy),
+            ["hit%d" % (LAST - 1), "hpad%d" % (LAST - 1), "lk4", "part%d" % LAST], [rmk], G1, 0)
+    turned(T.m1, "m1", T.part, LAST, i15, ["id2", "part%d" % LAST], True)
+    mm(T.m1[:], col(T.dm, LAST - 1, 128), rm4, False, False, ["dm", rmk], "m1", 0)
+    todo = list(range(RO + ahead, 16)) + [i for i in range(LAST) if i != r]
+    mm(fb, n256i, T.none[:], True, False, ["id3", "none", "relv"], fk, 2)
+
+    def acc(w, x, R, stop=False):
+        mms([(fb, w, x, False, stop)], R + ([] if stop else [fk]), [fk] if stop else [], 2)
+
+    def f_own():
+        acc(p128i, hit[r][:, 0:E], ["id4", "hit%d" % r])
+        acc(n256i, T.eqs[:], ["eqs"], r == LAST)
+
+    def differ(i, n):
+        bank, key = banks[n % 2] if n < M3 else banks[n % 3]
+        mms([(bank, md, col(T.zall, i), True, i >= LAST)] + ([(bank, p32i, col(T.rem, 2 * i + 1), False, True)] if i < LAST else []),
+            ["md", "zall", "id5", "relv"] + (["rem%d" % (2 * i + 1)] if i < LAST else []), [key])
+        return bank, key
+
+    acc(n256i, T.eqv[:], ["eqv"])
+    for i in range(RO, RO + ahead):
+        acc(p2i, col(T.eq, i), ["id6", "eq%d" % i])
+    if r < LAST:
+        f_own()
+        bank4, key4 = differ(LAST, 1)
+        vop(lambda: ve.tensor_scalar(col(T.eq, LAST), bank4, 0.0, None, A.is_equal), [], ["eq%d" % LAST, key4], E, 2)
+        acc(ident, col(T.eq, LAST), ["eq%d" % LAST])
+    for n, i in enumerate(todo):
+        bank, key = differ(i, n); c = n % 4
+        if n < 2:
+            vop(lambda bank=bank, c=c: ve.tensor_copy(col(T.eq, c), bank), [], ["eq%d" % c, key], E, 2)
+        else:
+            vop(lambda bank=bank, c=c: ve.tensor_tensor(col(T.eq, c), col(T.eq, c ^ 2), bank, A.mult), ["eq%d" % (c ^ 2)], ["eq%d" % c, key], E, 2)
+        if i < LAST:
+            acc(col(T.dm, i, 128), col(T.rem, 2 * i), ["dm", "rem%d" % (2 * i)])
+    for n in (len(todo) - 2, len(todo) - 1):
+        c = n % 4
+        vop(lambda c=c: ve.tensor_scalar(col(T.eq, c ^ 2), col(T.eq, c), 0.0, None, A.is_equal), ["eq%d" % c], ["eq%d" % (c ^ 2)], E // 2, 2)
+        acc(p2i, col(T.eq, c ^ 2), ["id6", "eq%d" % (c ^ 2)], r < LAST and n == len(todo) - 1)
+    if r < LAST:
+        aop(lambda: ac.activation(col(T.fp, 0), fb, F.Identity, bias=-128.0), [], ["fp0", fk], E, 0)
+    decide(LAST, col(T.pb0, 1), "pb0_1", T.red[:], "red")
+    if r == LAST:
+        f_own()
+        vop(lambda: ve.tensor_scalar(T.flag[:], fb, 128.5, None, A.is_gt), [], ["flag", fk], E, 0)
+    dma("sy", "dfl", [(T.yflag[:], T.flag[:])], ["flag"], [])
+    for k in range(LAST):
+        if k != r:
+            dma("sy", "do%d" % k, [(T.ysep[:, k * E:(k + 1) * E], col(T.sepc, k, 32))], ["sepc%d" % k], [])
+    return ops
+
+
+def order(ranks):
+    ext = {}
+    for ops in ranks:
+        for o in ops:
+            o["next"] = []
+            for k, keys, sem, n in o["sends"]:
+                for key in keys:
+                    ext[(k, key)] = o
+    cand = {}
+    for r, ops in enumerate(ranks):
+        lw = {}; rd = {}
+        for n, o in enumerate(ops):
+            pre = {}
+            for k in o["R"] + o["W"]:
+                p = lw.get(k) or ext.get((r, k))
+                if p is not None:
+                    pre[(p["r"], p.get("n", -1), k if p["r"] != r else "")] = p
+            for k in o["W"]:
+                for p in rd.get(k, []):
+                    pre[(r, p["n"], "")] = p
+            o["n"] = n; o["left"] = len(pre); o["ready"] = 0.0
+            o["key"] = (round(o["pr"]), n + 100 * (o["pr"] - round(o["pr"])))
+            for p in pre.values():
+                p["next"].append(o)
+            for k in o["R"]:
+                rd.setdefault(k, []).append(o)
+            for k in o["W"]:
+                lw[k] = o; rd[k] = []
+            cand.setdefault((r, o["q"]), [])
+            if not pre:
+                cand[(r, o["q"])].append(o)
+    free = {q: 0.0 for q in cand}; out = [[] for _ in ranks]; called = set()
+    while True:
+        best = None
+        for q, c in cand.items():
+            if c:
+                t0 = max(free[q], min(o["ready"] for o in c))
+                o = min((o for o in c if o["ready"] <= t0 + (SLACK if o["pr"] > 0 else URGENT)), key=lambda o: o["key"])
+                t = max(t0, o["ready"])
+                if best is None or t < best[0]:
+                    best = (t, q, o)
+        if best is None:
+            return out
+        t, q, o = best
+        cand[q].remove(o); out[q[0]].append(o)
+        free[q] = t + o["cost"] + (2500 if o["sends"] and q not in called else 0)
+        if o["sends"]:
+            called.add(q)
+        for x in o["next"]:
+            x["ready"] = max(x["ready"], free[q] + (0 if q == (x["r"], "pe") and x["q"] == "pe" else o["lat"] + HOP))
+            x["left"] -= 1
+            if x["left"] == 0:
+                cand[(x["r"], x["q"])].append(x)
 
 
 def rank_program(g, core, T, topo):
     r = T.rank_of(core)
     if r is None:
         return
+    ranks = [build(k, g, T, topo) for k in range(N)]
+    if not PLAN:
+        PLAN.extend([o["n"] for o in ops] for ops in order(ranks))
     Q = {"ve": g.vector, "ac": g.scalar, "pe": g.tensor, "po": g, "sy": g.sync}
     cnt = {}; waited = {q: {} for q in Q}; lw = {}; rd = {}
-    last = RO - 1
+    mine = [s for ops in ranks for o in ops for s in o["sends"] if s[0] == r]
+    for k, keys, sem, n in mine:
+        cnt[sem] = cnt.get(sem, 0) + n
+    for k, keys, sem, n in mine:
+        for key in keys:
+            lw[key] = (sem, cnt[sem])
 
     def need(q, tok):
-        if (q == "pe" and tok[0] == "pe") or waited[q].get(tok[0], 0) >= tok[1]:
-            return
-        Q[q].wait_ge(T.sem[tok[0]], tok[1]); waited[q][tok[0]] = tok[1]
+        if not (q == "pe" and tok[0] == "pe") and waited[q].get(tok[0], 0) < tok[1]:
+            Q[q].wait_ge(T.sem[tok[0]], tok[1]); waited[q][tok[0]] = tok[1]
 
-    def deps(q, R, W):
-        best = {}
-        for tok in [lw.get(k) for k in R] + [lw.get(k) for k in W] + [t for k in W for t in rd.get(k, [])]:
+    for o in [ranks[r][n] for n in PLAN[r]]:
+        if not o["fns"]:
+            continue
+        q = o["q"]; best = {}
+        for tok in [lw.get(k) for k in o["R"] + o["W"]] + [t for k in o["W"] for t in rd.get(k, [])]:
             if tok is not None and best.get(tok[0], 0) < tok[1]:
                 best[tok[0]] = tok[1]
         for s in best:
             need(q, (s, best[s]))
-
-    def mark(tok, R, W):
-        for k in R:
+        sem = o["sem"] or q
+        for fn in o["fns"]:
+            if sem == "ls":
+                fn(); cnt[sem] = cnt.get(sem, 0) + sum(s[3] for s in o["sends"])
+            else:
+                n = 16 if o["sem"] else 1
+                fn().then_inc(T.sem[sem], n); cnt[sem] = cnt.get(sem, 0) + n
+        tok = (sem, cnt[sem])
+        for k in o["R"]:
             rd.setdefault(k, []).append(tok)
-        for k in W:
+        for k in o["W"]:
             lw[k] = tok; rd[k] = []
-
-    def op(q, fn, R, W):
-        deps(q, R, W)
-        cnt[q] = cnt.get(q, 0) + 1
-        fn().then_inc(T.sem[q], 1)
-        mark((q, cnt[q]), R, W)
-
-    def dmas(q, sem, items):
-        tok = (sem, 16 * len(items)); cnt[sem] = tok[1]
-        for out, in_, R, W in items:
-            deps(q, R, W)
-            Q[q].dma_start(out, in_).then_inc(T.sem[sem], 16)
-        for out, in_, R, W in items:
-            mark(tok, R, W)
-
-    others = [k for k in range(N) if k != r]
-    eng = topo.engines(core, T.cores[others[0]])
-    share = len(eng) // len(others)
-
-    def dst(k):
-        rid, pid, se = topo.addr(T.cores[k])
-        return DstId(rid=rid, pnc=pid)
-
-    def bcast(ap, keys, sem, to=None):
-        deps("po", keys, [])
-        tr = []
-        for n, k in enumerate(others):
-            m = sum(1 << e for e in topo.engines(core, T.cores[k])[n::len(others)])
-            tr.append(RemoteDMATransfer(dst_ids=[dst(k)], dma_engine_mask=m, remote_sem=T.sem[sem], src=ap, dst=ap if to is None else to))
-        g.remote_dma_fused(tr, local_sem=T.sem.ls)
-        cnt["ls"] = cnt.get("ls", 0) + share * len(others)
-
-    def send_part(t):
-        deps("po", ["part%d" % t], [])
-        rid, pid, se = topo.addr(T.cores[t])
-        g.remote_dma(T.land[:, r * E:(r + 1) * E], T.part[:, t * E:(t + 1) * E], T.sem.arp, T.sem.ls, pid, rid, topo.mask(core, T.cores[t]))
-        cnt["ls"] = cnt.get("ls", 0) + len(eng)
-
-    def arrives(keys, sem, n):
-        cnt[sem] = n
-        for key in keys:
-            lw[key] = (sem, n)
-
-    if r < last:
-        arrives(["land%d" % k for k in others], "arp", len(eng) * len(others))
-        arrives(["zc2"], "arz", share)
-        arrives(["lk4"], "ark", share)
-    for k in others:
-        arrives(["tic%d" % k], "art%d" % k, share)
-        arrives(["lanq%d" % k], "arq%d" % k, share)
-        if k < last:
-            arrives(["hit%d" % k], "arh%d" % k, share)
-            arrives(["sepc%d" % k], "ars%d" % k, share)
-        if k > 0:
-            arrives(["off%d_%d" % (k, i) for i in range(18)], "arl%d" % k, share)
-
-    ve, ac, pe = g.vector, g.scalar, g.tensor
-    col = lambda buf, k, w=E: buf[:, k * w:(k + 1) * w]
-    lst = lambda t, i, n=1: T.off[:, t * LW + 32 * i:t * LW + 32 * (i + n)]
-    xw = T.xs[:, 0:V + 16]
-    ident, nid, n128i, p128i, p8ki, n1536i = [col(T.idm, k, 128) for k in range(6)]
-    hit = [T["hit%d" % k] for k in range(5)]
-    own = 0 if r == 0 else 2 if r == last else 1
-    z16, p16, zk = col(T.zc, own), col(T.pc, 1), "zc%d" % own
-
-    def mm(out, lhsT, rhs, start, stop, R, bank):
-        op("pe", lambda: pe.matmul(out, lhsT, rhs, start, stop), R, [bank])
-
-    ob = T.onesb[:, 0:128]
-    dmas("ac", "dtv", [(T.tvs[:], T.tv[:], [], ["tvs"])])
-    dmas("sy", "dx", [(T.xs[:, 0:V], T.x[:], [], ["xs"])])
-    op("ve", lambda: ve.memset(T.adj0[:], 0), [], ["adj0"])
-    dmas("sy", "dadj0", [(T.adj0[t::16, :], T.adj[t::16, :], ["adj0"], ["adr%d" % t]) for t in sorted({0, r})])
-    dmas("sy", "dadj", [(T.adjs[:], T.adj[:], [], ["adjs"])])
-    op("ve", lambda: ve.memset(ob, 1.0), [], ["ob"])
-    for q in range(2):
-        for gl in range(2):
-            op("po", lambda: g.affine_select(col(T.sw, 2 * q + gl, 128), ob, [[-32, 4], [128, 2], [-1, 16]], A.is_equal, 0.0,
-                                             -16 * q - 128 * gl, 1), ["ob"], ["sw%d" % (2 * q + gl)])
-    op("po", lambda: g.affine_select(ident, ob, [[-1, 128]], A.is_equal, 0.0, 0, 1), ["ob"], ["id0"])
-    op("po", lambda: g.affine_select(T.g0[:], ob, [[-16, 8], [0, 16]], A.is_ge, 0.0, 0, 1), ["ob"], ["g0"])
-    op("po", lambda: g.affine_select(T.gm[:], T.g0[:], [[16, 8], [0, 16]], A.is_ge, 0.0, 15, -1), ["g0"], ["gm"])
-    op("po", lambda: g.iota(T.io2[:], [[1, E]], 0, 0, allow_small_or_imprecise_dtypes=True), [], ["io2"])
-    for t in sorted({0, r}):
-        op("ve", lambda: ve.tensor_copy(lst(t, 16), T.tvs[:, 32 * t:32 * t + 32]), ["tvs"], ["off%d_16" % t])
-    op("ve", lambda: ve.memset(T.xs[:, V:V + 16], 0.0), [], ["xpad"])
-    op("ve", lambda: ve.memset(T.n128[:], -128.0), [], ["n128"])
-    op("ve", lambda: ve.memset(T.red[:], 0.0), [], ["red"])
-    for k in sorted({r, last}):
-        op("ve", lambda: ve.memset(hit[k][:, E:E + 16], 0.0), [], ["hpad%d" % k])
-    op("ac", lambda: ac.activation(T.ti[:], T.xs[:, 0:V], F.Identity, bias=float(E), scale=0.0), ["xs"], ["ti"])
-
-    def rows(dstb, win, wkey, l, lkey, key):
-        op("ve", lambda: ve.tensor_scalar(dstb, win.indirect(l), -float(OFS), None, A.add), [wkey, lkey], [key])
-
-    def swap(bank, c0, src, i, n, key, bkey):
-        for q in range(2):
-            for gl in range(2):
-                mm(bank[:, c0 + q:c0 + 2 * n:2], col(T.sw, 2 * q + gl, 128), src[:, 16 * gl + i::32], gl == 0, gl == 1,
-                   ["sw%d" % (2 * q + gl), key], bkey)
-
-    def turn(dstb, src, key, dkey):
-        op("ve", lambda: ve.transpose(dstb, src), [key], [dkey])
-
-    def tolist(t, i, n, bank, c0, bkey):
-        op("ve", lambda: ve.tensor_scalar(lst(t, i, n), bank[:, c0:c0 + 32 * n], float(OFS), None, A.add), [],
-           ["off%d_%d" % (t, j) for j in range(i, i + n)] + [bkey])
-
-    aw = T.adjs[:, 0:V]
-
-    def prep(t, k):
-        c = t % 2
-        if k == 0:
-            op("ac", lambda: ac.activation(col(T.xy, c), xw.indirect(lst(t, 17)), F.Copy), ["xs", "xpad", "off%d_17" % t], ["xy%d" % c])
-        if k == 1:
-            op("ve", lambda: ve.tensor_tensor(col(T.dd, c), xw.indirect(lst(t, 16)), col(T.xy, c), A.subtract),
-               ["xs", "xpad", "off%d_16" % t, "xy%d" % c], ["dd%d" % c])
-            op("ac", lambda: ac.activation(col(T.ad, c), col(T.dd, c), F.Abs), ["dd%d" % c], ["ad%d" % c])
-        if k == 2:
-            op("ve", lambda: ve.tensor_tensor(col(T.lo, c), xw.indirect(lst(t, 16)), col(T.xy, c), A.min),
-               ["xs", "xpad", "off%d_16" % t, "xy%d" % c], ["lo%d" % c])
-        if k == 3:
-            op("ve", lambda: ve.tensor_scalar(col(T.dl, c), col(T.ad, c), 0.5, -1.0, A.max, A.mult), ["ad%d" % c], ["dl%d" % c])
-
-    rows(col(T.pc, 0), T.adj0[:, 0:V], "adr0", lst(0, 16), "off0_16", "pc0")
-    turn(col(T.pt, 0), col(T.pc, 0), "pc0", "pt0")
-    swap(T.m1, 0, col(T.pt, 0), 0, 16, "pt0", "m1")
-    for k, c in ((1, -1.0), (2, -128.0), (3, 128.0)):
-        op("ve", lambda: ve.tensor_scalar(col(T.idm, k, 128), ident, c, None, A.mult), ["id0"], ["id%d" % k])
-    tolist(0, 17, 1, T.m1, 0, "m1")
-    prep(0, 0)
-    for k, c in ((4, 8192.0), (5, -float(OFS))):
-        op("ve", lambda: ve.tensor_scalar(col(T.idm, k, 128), ident, c, None, A.mult), ["id0"], ["id%d" % k])
-    op("ve", lambda: ve.tensor_scalar(T.ngm[:], T.gm[:], -1.0, None, A.mult), ["gm"], ["ngm"])
-    op("po", lambda: g.affine_select(T.u0[:], T.ngm[:], [[1, 128]], A.is_gt, 0.0, 0, -1), ["ngm"], ["u0"])
-    op("po", lambda: g.affine_select(T.dm[:], T.n128[:], [[-128, 5], [-16, 8], [128, 16]], A.is_equal, 0.0, 0, 1), ["n128"], ["dm"])
-    if own:
-        rows(p16, T.adj0[:, 0:V], "adr0", lst(r, 16), "off%d_16" % r, "p16")
-        turn(col(T.pt, 1), p16, "p16", "pt1")
-        swap(T.m1, 0, col(T.pt, 1), r, 16, "pt1", "m1")
-    prep(0, 1); prep(0, 2)
-    if own:
-        tolist(r, 17, 1, T.m1, 0, "m1")
-    prep(0, 3)
-    op("ac", lambda: ac.activation(T.onesb[:, 128:2048], T.xs[:, 128:2048], F.Identity, bias=1.0, scale=0.0), ["xs"], ["onesb"])
-    op("po", lambda: g.affine_select(T.bm[:], T.onesb[:], [[-1, 16], [-16, 8], [0, 16]], A.is_equal, 0.0, 0, 1), ["ob", "onesb"], ["bm"])
-    rows(col(T.zc, 0), aw, "adjs", lst(0, 17), "off0_17", "zc0")
-    turn(col(T.zt, 0), col(T.zc, 0), "zc0", "zt0")
-    for i in range(1, 5):
-        swap(T.m2, 32 * i, col(T.zt, 0), i, 16, "zt0", "m2")
-    for i in range(5, 16):
-        swap(T.m3, 32 * i, col(T.zt, 0), i, 16, "zt0", "m3")
-    if own:
-        rows(z16, aw, "adjs", lst(r, 17), "off%d_17" % r, zk)
-    tolist(0, 1, 4, T.m2, 32, "m2")
-
-    def x_rest():
-        tolist(0, 5, 11, T.m3, 160, "m3")
-        if own:
-            turn(col(T.zt, 1), z16, zk, "zt1")
-            for i in range(8):
-                swap(T.m2, 32 * i, col(T.zt, 1), i, 16, "zt1", "m2")
-
-    def x_p():
-        rows(p16, aw, "adjs", lst(r, 16), "off%d_16" % r, "p16")
-
-    def x_z2():
-        if own:
-            for i in range(8, 16):
-                swap(T.m2, 32 * i, col(T.zt, 1), i, 16, "zt1", "m2")
-
-    def x_lists():
-        if own:
-            tolist(r, 0, 16, T.m2, 0, "m2")
-            bcast(lst(r, 0, 18), ["off%d_%d" % (r, i) for i in (0, 16, 17)], "arl%d" % r)
-
-    def x_scatter(h):
-        op("ve", lambda: ve.tensor_copy(T.ti[:, 0:V].indirect(lst(r, 16 + h)), T.io2[:]), ["io2", "off%d_%d" % (r, 16 + h)], ["ti"])
-        if h == 0:
-            return
-        dmas("sy", "dtc", [(col(T.tic, r, 192), T.ti[r::16, :], ["ti"], ["tic%d" % r])])
-        bcast(col(T.tic, r, 192), ["tic%d" % r], "art%d" % r)
-        if r == last:
-            bcast(z16, [zk], "arz")
-        deps("sy", [], ["ti"])
-        dmas("sy", "dtr", [(T.ti[k::16, :], col(T.tic, k, 192), ["tic%d" % k], ["tir%d" % k]) for k in others])
-
-    def x_static():
-        op("ve", lambda: ve.tensor_tensor(T.um[:], T.u0[:], ident, A.add), ["u0", "id0"], ["um"])
-        op("ve", lambda: ve.tensor_scalar(T.none[:], z16, V - OFS - 0.5, None, A.is_ge), [zk], ["none"])
-        mm(T.m3[:], col(T.bm, r, 128), z16, True, True, ["bm", zk], "m3")
-
-    def x_eqv():
-        op("ve", lambda: ve.tensor_tensor(T.eqv[:], z16, T.m3[:], A.is_equal), [zk], ["eqv", "m3"])
-
-    def x_link():
-        op("ve", lambda: ve.tensor_copy(T.lk[:], T.ti[:, 0:V].indirect(lst(r, 16, 2))),
-           ["ti", "off%d_16" % r, "off%d_17" % r] + ["tir%d" % k for k in others], ["lk"])
-        turn(T.lt[:], T.lk[:], "lk", "lt")
-        for k in range(RO):
-            swap(T.m3, 64 * k, T.lt, k, 32, "lt", "m3")
-
-    def x_linkl():
-        op("ve", lambda: ve.tensor_copy(T.lkl[:], T.m3[:, 0:320]), [], ["lkl", "m3"])
-        if r == last:
-            bcast(col(T.lkl, 2 * last - 1, 32), ["lkl"], "ark", T.lk4[:])
-
-    def x_rem(k, side, n=1):
-        j = 2 * k + side
-        op("ac", lambda: ac.activation(T.rem[:, j * E:(j + n) * E], hit[k][:, 0:E + 16].indirect(T.lkl[:, 32 * j:32 * (j + n)]), F.Copy),
-           ["hit%d" % k, "hpad%d" % k, "lkl"], ["rem%d" % (j + d) for d in range(n)])
-
-    def sums(t, k, start, stop):
-        buf, c, key = (T.part, t, "part%d" % t) if k == r else (T.lanq, k, "lanq%d" % k) if t == last else (T.land, k, "land%d" % k)
-        for blk in range(4):
-            mm(col(T.m1, blk, 128), buf[:, c * E + 128 * blk:c * E + 128 * blk + 128], ident, start and blk == 0, stop and blk == 3, [key], "m1")
-
-    def d_pre():
-        mm(T.m1[:], n128i, T.eqv[:], True, False, ["id2", "eqv"], "m1")
-        mm(T.m1[:], n128i, T.none[:], False, False, ["id2", "none"], "m1")
-        sums(r, r, False, False)
-        for k in range(r):
-            mm(T.m1[:], col(T.dm, k, 128), col(T.rem, 2 * k + 1), False, False, ["dm", "rem%d" % (2 * k + 1)], "m1")
-
-    def x_pen():
-        terms = [(T.eqv, 0, n128i, "eqv"), (T.none, 0, n128i, "none")] + [
-            (T.rem, (2 * k + 1) * E, col(T.dm, k, 128), "rem%d" % (2 * k + 1)) for k in range(last - 1)]
-        for blk in range(4):
-            for n, (buf, c0, w, key) in enumerate(terms):
-                mm(col(T.m1, blk, 128), buf[:, c0 + 128 * blk:c0 + 128 * blk + 128], w, n == 0, n == len(terms) - 1, [key, "dm", "id2"], "m1")
-        op("ac", lambda: ac.activation(T.pen[:], T.m1[:], F.Copy), [], ["pen", "m1"])
-
-    def d_sum(t):
-        for k in others:
-            sums(t, k, False, k == others[-1])
-        op("ac", lambda: ac.activation(T.absa[:], T.m1[:], F.Abs, bias=float(16 * N)), [], ["absa", "m1"])
-
-    def d_ok(t):
-        op("ve", lambda: ve.tensor_scalar(T.ok[:], T.absa[:], 10.5, None, A.is_le), ["absa"], ["ok"])
-        mm(T.m1[:], T.gm[:], T.ok[:], True, True, ["gm", "ok"], "m1")
-        mm(T.m2[:], T.um[:], T.ok[:], True, True, ["um", "ok"], "m2")
-        op("ac", lambda: ac.activation(hit[t][:, 0:E], T.m1[:], F.Sign), [], ["hit%d" % t, "m1"])
-        if t < last:
-            bcast(hit[t][:], ["hpad%d" % t, "hit%d" % t], "arh%d" % t)
-
-    def d_first(t):
-        z, key = (col(T.zc, 2), "zc2") if t == last else (z16, zk)
-        op("ve", lambda: ve.tensor_scalar(T.first[:], T.m2[:], 0.0, None, A.max), [], ["first", "m2"])
-        op("ve", lambda: ve.tensor_tensor(T.mz[:], T.first[:], z, A.mult), ["first", key], ["mz"])
-        if t == r:
-            mm(T.m3[:], T.gm[:], T.mz[:], True, True, ["mz"], "m3")
-        mm(T.m2[:], T.gm[:], T.mz[:], True, False, ["mz"], "m2")
-        mm(T.m2[:], n1536i, hit[t][:, 0:E], False, True, ["id5", "hit%d" % t], "m2")
-
-    def d_sep(t):
-        c = int(t == last); sp = T.sep[0::16, c * E:(c + 1) * E]
-        op("ac", lambda: ac.activation(col(T.sep, c), T.m2[:], F.Identity, bias=float(V)), [], ["sep%d" % c, "m2"])
-        if t < last:
-            dmas("sy", "dsc", [(col(T.sepc, t, 32), sp, ["sep0"], ["sepc%d" % t])])
-        dmas("ac" if c else "sy", "do%d" % t, [(T.ysep[:, t * E:(t + 1) * E], sp, ["sep%d" % c], [])])
-
-    def d_send(t):
-        bcast(col(T.sepc, t, 32), ["sepc%d" % t], "ars%d" % t)
-
-    def d_eqs():
-        op("ve", lambda: ve.tensor_tensor(T.eqs[:], z16, T.m3[:], A.is_equal), [zk], ["eqs", "m3"])
-
-    def x_out(k):
-        if k != r:
-            dmas("sy", "do%d" % k, [(T.ysep[:, k * E:(k + 1) * E], col(T.sepc, k, 32), ["sepc%d" % k], [])])
-
-    def bc(i, bank, key, masked):
-        mm(bank, col(T.bm, i, 128), p16, True, not masked, ["bm", "p16"], key)
-        if masked:
-            mm(bank, p8ki, col(T.rem, 2 * i), False, True, ["id4", "rem%d" % (2 * i)], key)
-
-    def eq(i, bank, key):
-        op("ve", lambda: ve.tensor_tensor(col(T.eq, i), z16, bank, A.is_equal), [zk], ["eq%d" % i, key])
-
-    units = []; base = []
-    for t in range(RO):
-        sl = [i for i in range(16) if i != t]; base.append(len(units))
-        for u in UNITS[t].split():
-            units.append((t, sl[:int(u[1])], u[0])); sl = sl[int(u[1]):]
-    S = len(units)
-    extra = {}
-
-    def at(t, u, *fns):
-        extra.setdefault((base[t] if u >= 0 else (base + [S])[t + 1]) + u, []).extend(fns)
-
-    at(0, 1, x_rest); at(0, 2, x_z2); at(0, 4, x_lists); at(0, 5, lambda: x_scatter(0)); at(0, 7, lambda: x_scatter(1))
-    at(1, 0, x_p); at(1, 1, x_static); at(1, 2, x_eqv); at(1, 6, x_link); at(1, 8, x_linkl)
-    for t in range(1, RO):
-        for k, u in enumerate((-4, -2, -2, -1)):
-            at(t - 1, u, lambda t=t, k=k: prep(t, k))
-    for k in range(r):
-        if k + 2 <= last:
-            at(k + 2, 6 if k + 1 == r else 7 if k + 2 == last else 8, lambda k=k: x_rem(k, 1))
-    if r < last - 1:
-        at(r + 1, 7, d_pre, lambda: d_sum(r)); at(r + 1, 8, lambda: d_ok(r))
-        at(r + 2, 0, lambda: d_first(r), lambda: d_sep(r)); at(r + 2, 2, d_eqs); at(r + 2, 3, lambda: d_send(r))
-    elif r < last:
-        at(last, 7, d_pre, lambda: d_sum(r)); at(last, 8, lambda: d_ok(r)); at(last, 9, lambda: d_first(r), lambda: d_sep(r), d_eqs)
-    else:
-        at(last, 8, x_pen)
-    mb = [(T.m2[:], "m2"), (T.m3[:], "m3")]
-    todo = ([last] if r < last else []) + list(range(RO, 16)) + [i for i in range(last) if i != r]
-    for k in range(RO - 2):
-        at(k + 2, 6, lambda k=k: x_out(k))
-
-    DR = 4
-
-    def drain():
-        for n in range(DR - 2):
-            eq(todo[n], mb[n % 2][0], mb[n % 2][1]); bc(todo[n + 2], mb[n % 2][0], mb[n % 2][1], False)
-
-    extra.setdefault(S - 1, []).extend([lambda n=n: bc(todo[n], mb[n % 2][0], mb[n % 2][1], False) for n in (0, 1)])
-    extra.setdefault(S, []).append(drain)
-
-    def gat_v(s):
-        t, sl, kind = units[s]; c = t % 2; a = s % NA
-        for j, i in enumerate(sl):
-            op("ve", lambda: ve.tensor_tensor(col(T.ab, 2 * a + j), xw.indirect(lst(t, i)), col(T.lo, c), A.subtract),
-               ["xs", "xpad", "off%d_%d" % (t, i), "lo%d" % c], ["ab%d_%d" % (a, j)])
-        if kind == "v":
-            w = slice(1024 * a, 1024 * a + E * len(sl))
-            op("ve", lambda: ve.tensor_scalar(T.sa[:, w], T.ab[:, w], -1.0, 1.0, A.max, A.min),
-               ["ab%d_%d" % (a, j) for j in range(len(sl))], ["sa%d" % a])
-
-    def gat_s(s):
-        t, sl, kind = units[s]; a = s % NA
-        op("ac", lambda: ac.activation(col(T.ab, 2 * a), xw.indirect(lst(t, sl[0])), F.Copy),
-           ["xs", "xpad", "off%d_%d" % (t, sl[0])], ["ab%d_0" % a])
-
-    def pe_b(s):
-        t, sl, kind = units[s]; c = t % 2; a = s % NA; pb = T["pb%d" % (s % 2)]; kb = "pb%d_" % (s % 2)
-        if kind == "s":
-            for j in range(2):
-                mm(col(pb, j), nid, col(T.lo, c), True, False, ["id1", "lo%d" % c], kb + str(j))
-                if j == 0:
-                    mm(col(pb, j), ident, col(T.dl, c), False, False, ["dl%d" % c], kb + str(j))
-                mm(col(pb, j), ident, col(T.ab, 2 * a), False, True, ["id0", "ab%d_0" % a], kb + str(j))
-            return
-        for j in range(len(sl)):
-            mm(col(pb, j), ident, col(T.dl, c), True, False, ["id0", "dl%d" % c], kb + str(j))
-            mm(col(pb, j), ident, col(T.ab, 2 * a + j), False, True, ["ab%d_%d" % (a, j)], kb + str(j))
-
-    def sign_b(s):
-        t, sl, kind = units[s]; n = 2 if kind == "s" else len(sl); b = s % NS
-        op("ac", lambda: ac.activation(T.sb[:, 1024 * b:1024 * b + E * n], T["pb%d" % (s % 2)][:, 0:E * n], F.Sign),
-           [], ["sb%d" % b] + ["pb%d_%d" % (s % 2, j) for j in range(n)])
-
-    def sign_a(s):
-        t, sl, kind = units[s]; a = s % NA; w = slice(1024 * a, 1024 * a + E * len(sl))
-        op("ac", lambda: ac.activation(T.sa[:, w], T.ab[:, w], F.Sign), ["ab%d_%d" % (a, j) for j in range(len(sl))], ["sa%d" % a])
-
-    def pe_r(s):
-        t, sl, kind = units[s]; a = s % NA; b = s % NS
-        for j, i in enumerate(sl):
-            for blk in range(4):
-                o = T.red[:, 128 * blk + i:128 * blk + 128:16]; c0 = E * j + 128 * blk
-                if kind == "s":
-                    mm(o, T.sb[:, 1024 * b + E + c0:1024 * b + E + c0 + 128], T.ngm[:, 0::16], True, False, ["sb%d" % b, "ngm"], "red")
-                else:
-                    mm(o, T.sa[:, 1024 * a + c0:1024 * a + c0 + 128], T.ngm[:, 0::16], True, False, ["sa%d" % a, "ngm"], "red")
-                mm(o, T.sb[:, 1024 * b + c0:1024 * b + c0 + 128], T.gm[:, 0::16], False, True, ["sb%d" % b, "gm"], "red")
-
-    def evac(t):
-        op("ac", lambda: ac.activation(col(T.part, t), T.red[:], F.Copy), [], ["part%d" % t, "red"])
-        if t != r:
-            send_part(t)
-
-    for s in range(S + 1):
-        for fn in extra.get(s, []):
-            fn()
-        if s < S and units[s][2] != "s":
-            gat_v(s)
-        if s + 1 < S and units[s + 1][2] == "s":
-            gat_s(s + 1)
-        if s < S:
-            pe_b(s)
-        if s >= 1:
-            sign_b(s - 1)
-        if s >= 2 and s - 1 in base:
-            evac(units[s - 2][0])
-        if s < S and units[s][2] == "m":
-            sign_a(s)
-        if s >= 1:
-            pe_r(s - 1)
-
-    fb, fk = col(T.pb0, 0), "pb0_0"
-    banks = [(col(T.pb0, 1), "pb0_1"), (col(T.pb1, 0), "pb1_0"), (col(T.pb1, 1), "pb1_1")]
-    pos = [DR, DR]
-
-    def acc(i):
-        mm(fb, ident, col(T.eq, i), False, False, ["eq%d" % i], fk)
-
-    def ahead(n):
-        while pos[0] < min(n, len(todo)):
-            bc(todo[pos[0]], banks[pos[0] % 3][0], banks[pos[0] % 3][1], todo[pos[0]] < last); pos[0] += 1
-
-    def eqs(n):
-        for _ in range(n):
-            if pos[1] < len(todo):
-                ahead(pos[1] + 2)
-                eq(todo[pos[1]], banks[pos[1] % 3][0], banks[pos[1] % 3][1])
-                if pos[1] > DR:
-                    acc(todo[pos[1] - 1])
-                pos[1] += 1
-                if pos[1] == len(todo):
-                    acc(todo[-1])
-
-    def f_rem(k, stop):
-        mm(fb, col(T.dm, k, 128), col(T.rem, 2 * k + 1), False, stop, ["dm", "rem%d" % (2 * k + 1)], fk)
-
-    def f_own(stop):
-        mm(fb, p128i, hit[r][:, 0:E], False, False, ["id3", "hit%d" % r], fk)
-        mm(fb, n128i, T.eqs[:], False, stop, ["eqs"], fk)
-
-    for n in range(DR - 2, DR):
-        eq(todo[n], mb[n % 2][0], mb[n % 2][1])
-    if r == last:
-        op("ve", lambda: ve.tensor_tensor(col(T.part, last), T.red[:], T.pen[:], A.add), ["pen"], ["part%d" % last, "red"])
-    else:
-        op("ac", lambda: ac.activation(col(T.part, last), T.red[:], F.Copy), [], ["part%d" % last, "red"])
-    bcast(col(T.part, last), ["part%d" % last], "arq%d" % r, col(T.lanq, r))
-    if r == last - 1:
-        d_send(r)
-    for k in range(last - 1):
-        if k != r:
-            x_rem(k, 0, 2 if k > r else 1)
-    rm4, rmk = col(T.rem, 2 * last - 1), "rem%d" % (2 * last - 1)
-    if r < last:
-        rm4, rmk = T.rm4[:], "rm4"
-        op("ac", lambda: ac.activation(rm4, hit[last - 1][:, 0:E + 16].indirect(T.lk4[:]), F.Copy),
-           ["hit%d" % (last - 1), "hpad%d" % (last - 1), "lk4"], [rmk])
-    if r != last - 1:
-        x_rem(last - 1, 0, 2)
-    ahead(DR + 2)
-    mm(fb, n128i, T.none[:], True, False, ["none"], fk)
-    for i in todo[:DR]:
-        if i != last:
-            acc(i)
-    if r < last:
-        f_own(False)
-    x_out(last - 1)
-    eqs(TAIL[0])
-    mm(T.m1[:], col(T.dm, last - 1, 128), rm4, True, False, ["dm", rmk], "m1")
-    sums(last, r, False, False)
-    d_sum(last); eqs(TAIL[1]); d_ok(last); eqs(TAIL[2])
-    for k in range(last):
-        if k != r:
-            f_rem(k, False)
-    if r < last:
-        x_rem(last, 1)
-        eqs(16)
-        op("ve", lambda: ve.tensor_tensor(col(T.eq, 16), hit[last][:, 0:E + 16].indirect(col(T.lkl, 2 * last, 32)), col(T.eq, last), A.is_lt),
-           ["hit%d" % last, "hpad%d" % last, "lkl", "eq%d" % last], ["eq16"])
-        acc(16); f_rem(last, True)
-        d_first(last)
-    else:
-        d_first(last); eqs(16); d_eqs(); f_own(True)
-    op("ve", lambda: ve.tensor_scalar(T.flag[:], fb, 128.5, None, A.is_gt), [], ["flag", fk])
-    d_sep(last)
-    dmas("sy", "dfl", [(T.yflag[:], T.flag[:], ["flag"], [])])
     for s in cnt:
         need("po", (s, cnt[s]))

@@ -4,34 +4,35 @@ from concourse.mybir import AluOpType as A, ActivationFunctionType as F
 V, E, RO, N = 3072, 512, 5, 5
 LAST = RO - 1
 LW = 18 * 32
-OFS = 1536
+OFS = 2048
 BIG = 1.5 * 2 ** 28
-NA, NG = 4, 3
-UNITS = ["s1 v2 m2 s1 v2 v2 s1 v2 v2"] * 2 + ["s1 v2 m2 v2 s1 v2 m2 v2 v1"] * 2 + ["s1 v2 v2 v2 v2 v2 v2 v2"]
+NA, NG = 4, 2
+UNITS = ["s1 v2 v2 s1 v2 m2 v2 s1 v2", "s1 v2 m2 v2 s1 v2 m2 v2 v1", "s1 v2 v2 m2 s1 v2 v2 m2 v1", "s1 v2 m2 v2 s1 v2 m2 v2 v1"]
+ENDS = ["s1 v2 s1 v2 v2 v2 v2 v2 v1"] + ["s1 v2 v2 v2 v2 v2 v2 v2"] * 3 + ["s1 v2 s1 v2 v2 v2 v2 v2 v1"]
 EARLY = [0, 4, 4, 4, 2]
 EQ4 = 6
-PREP = 5
-FREE_V, FREE_A = 1, 6
-M3, REDP, DLAT, GPR = 8, 1.3, 3000, 1
-CY, PC, GA, SC, HOP, SLACK, URGENT, MARGIN = 0.9, 0.44, 1.5, 3.5, 120, 100, 150, 2000
-LATE = (6000, 3500, 2000, 500, 2500, 1500, 1000, 300)
+QUIET = 13
+PREP = 6
+FREE_V, FREE_A = 2, [2, 6, 6, 6, 8]
+M3, REDP = 2, 1.3
+CY, PC, GA, SC, HOP, SLACK, URGENT, MARGIN = 0.87, 0.46, 1.6, 3.5, 120, 100, 150, 2000
+LATE = (7000, 4500, 2500, 1000, 3500, 2500, 1000, 800)
 BF, F16, F32 = "bfloat16", "float16", "float32"
 SB = {"adjs": (V, "int32"), "adj0": (V, "int32"), "xs": (V + 16, BF), "tvs": (160, "int32"), "vl": (160, "uint16"),
-      "ti": (V, F32), "tic": (5 * 192, F32), "io2": (E, F32), "onesb": (OFS, BF), "n256": (E, BF), "sw": (E, BF),
-      "idm": (9 * 128, BF), "gm": (9 * 128, BF), "cm": (256, BF), "dm": (E, BF), "bm": (2048, BF),
+      "ti": (V, F32), "tic": (5 * 192, F32), "io2": (E, F32), "onesb": (V // 2, BF), "n256": (128, BF), "sw": (E, BF),
+      "idm": (9 * 128, BF), "gm": (9 * 128, BF), "cm": (256, BF), "dm": (640, BF), "bm": (2048, BF),
       "py": (E, F16), "pc": (E, F16), "pt": (E, F16), "zc": (2 * E, F16), "zt": (E, F16), "zall": (16 * E, F16),
-      "off": (5 * LW, "uint16"), "none": (E, BF), "eqv": (E, BF), "lk": (1024, F16), "lt": (1024, F16),
-      "lkl": (320, "uint16"), "rem": (8 * E, BF), "lk4": (32, "uint16"), "rm4": (E, BF),
-      "xv": (5 * E, BF), "xy": (2 * E, BF), "ad": (E, BF), "lo": (10 * E, BF), "dl": (10 * E, BF),
-      "ab": ((NA + NG) * 1024, BF), "sa": ((NA + NG) * 1024, BF), "sb": ((NA + NG) * 1024, BF),
+      "off": (5 * LW, "uint16"), "eqv": (E, BF), "lk": (1024, F16), "lt": (1024, F16),
+      "lkl": (320, "uint16"), "rem": (9 * E, BF), "lk4": (32, "uint16"), "rm4": (E, BF),
+      "xv": (5 * E, BF), "xy": (2 * E, BF), "ad": (E, BF), "lo": (10 * E, BF), "dl": (5 * E, BF),
+      "ab": ((NA + NG) * 1024, BF), "sa": ((NA + NG) * 1024, BF), "sb": (NA * 1024, BF),
       "part": (6 * E, BF), "land": (5 * E, BF), "lanq": (5 * E, BF), "ok": (E, BF), "mz": (E, F16),
-      "sep": (2 * E, F32), "sepc": (5 * 32, F32), "eqs": (E, BF), "eq": (16 * E, BF), "fp": (2 * E, BF), "flag": (E, BF)}
-SB.update({"hit%d" % k: (E + 16, BF) for k in range(6)})
+      "sep": (2 * E, F32), "sepc": (5 * 32, F32), "eqs": (E, BF), "eq": (16 * E, BF), "flag": (E, BF)}
+SB.update({"hit%d" % k: (E + 16, BF) for k in range(5)})
 SCRATCH = {k: ("sbuf", [128, w], d) for k, (w, d) in SB.items()}
 SCRATCH.update({k: ("psum", [128, w], F32) for k, w in (("pb0", 1024), ("pb1", 1024), ("pb2", 1024), ("red", E), ("m1", E))})
 SEMAPHORES = (["ve", "ac", "pe", "po", "ls", "arp", "arz", "ark", "arw6", "arw12", "dtv", "dadj", "dadj0", "dx", "dtc", "dtr", "dsc", "dfl"]
-              + ["%s%d" % (a, k) for a in ("do", "dd", "de", "dz", "ary", "arl", "art", "arh", "ars", "arq") for k in range(5)]
-              + ["da%d" % k for k in range(NA + NG)])
+              + ["%s%d" % (a, k) for a in ("do", "dz", "ary", "arl", "art", "arh", "ars", "arq") for k in range(5)])
 PLAN = []
 
 
@@ -71,22 +72,22 @@ def build(r, g, T, topo):
         tr = [RemoteDMATransfer(dst_ids=[dst(k)], dma_engine_mask=sum(1 << e for e in el[n]), remote_sem=T.sem[sem], src=ap,
                                 dst=ap if to is None else to) for n, k in enumerate(ranks)]
         add("po", [lambda: g.remote_dma_fused(tr, local_sem=T.sem.ls)], keys, [], 700, 0, 1600 + 1.5 * nbytes + margin, "ls",
-            [(k, tkeys or keys[:16], sem, len(el[n])) for n, k in enumerate(ranks)])
+            [(k, tkeys or keys, sem, len(el[n])) for n, k in enumerate(ranks)])
 
     col = lambda buf, k, w=E: buf[:, k * w:(k + 1) * w]
     lst = lambda t, i, n=1: T.off[:, t * LW + 32 * i:t * LW + 32 * (i + n)]
     lk_ = lambda t, i, n=1: ["off%d_%d" % (t, j) for j in range(i, i + n)]
     xw, aw, ob = T.xs[:, 0:V + 16], T.adjs[:, 0:V], T.onesb[:, 0:128]
-    ident, nid, i15, n256i, p128i, p32i, p2i, nsi, md = [col(T.idm, k, 128) for k in range(9)]
-    g0, gm, ngm, um, wm, gm4, w0, u0, w1 = [col(T.gm, k, 128) for k in range(9)]
-    hit = [T["hit%d" % k] for k in range(6)]
+    ident, nid, i15, n256i, p128i, p32i, g32, nsi, md = [col(T.idm, k, 128) for k in range(9)]
+    g0, gm, ngm, um, wm, hw, w0, u0, w1 = [col(T.gm, k, 128) for k in range(9)]
+    hit = [T["hit%d" % k] for k in range(5)]
     z16, p16, zk = col(T.zc, int(r == LAST)), T.pc[:], "zc%d" % int(r == LAST)
     G1 = GA * E; XS = ["xs", "xpad"]
 
     dma("ac", "dtv", [(T.tvs[:], T.tv[:])], [], ["tvs"], 1800)
     dma("sy", "dx", [(T.xs[:, 0:V], T.x[:])], [], ["xs"], 3600)
     vop(lambda: ve.memset(ob, 1.0), [], ["ob"], 64)
-    vop(lambda: ve.memset(T.onesb[:, 128:OFS], 1.0), [], ["onesb"], 704)
+    vop(lambda: ve.memset(T.onesb[:, 128:V // 2], 1.0), [], ["onesb"], 704)
     vop(lambda: ve.memset(T.adj0[:, 0:2048], 0), [], ["adja"], 2048)
     pop(lambda: g.iota(T.adj0[:, 2048:V], [[0, 1024]], 0, 0), [], ["adjb"], 1024)
     dma("sy", "dadj0", [(T.adj0[r::16, :], T.adj[r::16, :])], ["adja", "adjb"], ["adj0"], 1800)
@@ -96,7 +97,7 @@ def build(r, g, T, topo):
         aop(lambda: ac.activation(out, src, F.Identity, scale=float(scale)), R, [key], out.shape[1])
 
     for h in range(2):
-        const(col(T.ti, h, OFS), T.onesb[:], ["ob", "onesb"], "ti", E)
+        const(col(T.ti, h, V // 2), T.onesb[:], ["ob", "onesb"], "ti", E)
     pop(lambda: g.iota(T.io2[:], [[1, E]], 0, 0, allow_small_or_imprecise_dtypes=True), [], ["io2"], E)
     for n in range(4):
         pop(lambda n=n: g.affine_select(col(T.sw, n, 128), ob, [[-32, 4], [128, 2], [-1, 16]], A.is_equal, 0.0, -16 * (n // 2) - 128 * (n % 2), 1),
@@ -111,11 +112,10 @@ def build(r, g, T, topo):
     vop(lambda: ve.tensor_copy(T.vl[:], T.tvs[:]), ["tvs"], ["vl"], 160, 0)
     vop(lambda: ve.tensor_copy(lst(r, 17), T.tvs[:, 32 * r:32 * r + 32]), ["tvs"], lk_(r, 17), 64, 0)
     vop(lambda: ve.memset(T.xs[:, V:V + 16], 300.0), [], ["xpad"], 64)
-    vop(lambda: ve.memset(T.n256[:], -256.0), [], ["n256"], 256)
     vop(lambda: ve.memset(T.red[:], 0.0), [], ["red"], E)
-    vop(lambda: ve.memset(T.cm[:, 0:128], -12.0), [], ["cm0"], 64)
-    vop(lambda: ve.memset(T.cm[:, 128:256], 204.0), [], ["cm1"], 64)
-    for k in sorted({r, LAST, 5}):
+    vop(lambda: ve.memset(T.cm[:, 0:128], -16.0), [], ["cm0"], 64)
+    vop(lambda: ve.memset(T.cm[:, 128:256], 264.0), [], ["cm1"], 64)
+    for k in sorted({r, LAST}):
         vop(lambda k=k: ve.memset(hit[k][:, E:E + 16], 0.0), [], ["hpad%d" % k], 64)
 
     def scatter(h):
@@ -126,16 +126,18 @@ def build(r, g, T, topo):
         if n:
             aop(lambda t0=t0, n=n: ac.activation(T.xv[:, t0 * E:(t0 + n) * E], xw.indirect(T.vl[:, 32 * t0:32 * (t0 + n)]), F.Copy),
                 XS + ["vl"], ["xv%d" % t for t in range(t0, t0 + n)], n * G1, 0 if t0 == r else 1)
-    for k, c in enumerate((-1, 1.5, -256, 128, 32, 2, -1 / 256)):
+    for k, c in ((0, -1), (1, 1.5), (2, -256), (3, 128), (4, 32), (6, -1 / 256)):
         const(col(T.idm, k + 1, 128), ident, ["id0"], "id%d" % (k + 1), c)
     const(ngm, gm, ["gm"], "ngm", -1)
-    const(u0, gm, ["gm"], "u0", -2 * OFS)
+    const(u0, gm, ["gm"], "u0", -V)
+    const(T.n256[:], gm, ["gm"], "n256", -256)
+    const(g32, gm, ["gm"], "id6", 32)
     for c in ((0,), (1, 2))[r == LAST]:
         pop(lambda c=c: g.affine_select(col(T.bm, c), T.onesb[:, 0:E], [[-1, 4], [-16, 8], [0, 16]], A.is_equal, 0.0, -4 * c, 1),
             ["ob", "onesb"], ["bm%d" % c], E)
 
-    def rows(dstb, i, key, win=aw, wk="adjs", pr=0):
-        vop(lambda: ve.tensor_scalar(dstb, win.indirect(lst(r, i)), -float(OFS), None, A.add), [wk] + lk_(r, i), [key], G1, pr)
+    def rows(dstb, i, key, win=aw, wk="adjs", pr=0, top=V):
+        vop(lambda: ve.tensor_scalar(dstb, win.indirect(lst(r, i)), -float(OFS), float(top - OFS), A.add, A.min), [wk] + lk_(r, i), [key], G1, pr)
 
     def swap(bank, c0, src, i, n, key, bkey):
         mms([(bank[:, c0 + q:c0 + 2 * n:2], col(T.sw, 2 * q + gl, 128), src[:, 16 * gl + i::32], gl == 0, gl == 1) for q in range(2) for gl in range(2)],
@@ -162,11 +164,12 @@ def build(r, g, T, topo):
     if r == LAST:
         bcast(z16, [zk], "arz", 1024)
     pop(lambda: g.affine_select(um, u0, [[1, 128]], A.is_gt, 0.0, 0, -1), ["u0"], ["um"], 128)
-    pop(lambda: g.affine_select(um, um, [[-1, 128]], A.not_equal, 2.0 * OFS, 0, 1), [], ["um"], 128)
-    pop(lambda: g.affine_select(T.dm[:], T.n256[:], [[-128, 4], [-16, 8], [128, 16]], A.is_equal, 0.0, 0, 1), ["n256"], ["dm"], E)
+    pop(lambda: g.affine_select(um, um, [[-1, 128]], A.not_equal, float(V), 0, 1), [], ["um"], 128)
+    for k in range(RO):
+        pop(lambda k=k: g.affine_select(col(T.dm, k, 128), T.n256[:], [[0, 8], [1, 16]], A.is_equal, 0.0, -k, 0), ["n256"], ["dm"], 128)
     pop(lambda: g.iota(w0, [[-16, 8], [0, 16]], -14, 1, allow_small_or_imprecise_dtypes=True), [], ["w0"], 128)
     ingroup(w0, w0, "w0", "w0")
-    pop(lambda: g.affine_select(gm4, gm, [[0, 8], [1, 16]], A.is_equal, 0.0, -LAST, 0), ["gm"], ["gm4"], 128)
+    pop(lambda: g.affine_select(hw, p128i, [[-16, 8], [0, 16]], A.not_equal, 0.0, -r, 1), ["id4"], ["hw"], 128)
 
     seen = {"a": 0, "p": 0, "s": 0}
 
@@ -186,10 +189,8 @@ def build(r, g, T, topo):
         mms([(col(pb, 1), ident, xv, True, False), (col(pb, 1), nid, xy, False, True)], ["id1", kv, ky], [kb[1]], -1)
         vop(lambda: ve.tensor_tensor(lo, xy, col(pb, 0), A.min), [ky], ["lo%d" % t, kb[0]], E, -1)
         aop(lambda: ac.activation(T.ad[:], col(pb, 1), F.Abs), [], ["ad", kb[1]], E, -1)
-        vop(lambda: ve.tensor_scalar(col(T.dl, 2 * t), T.ad[:], 0.5, -1.0, A.max, A.mult), ["ad"], ["dl%d" % t], E // 2, -1)
-        for kind, buf, key in (("d", T.dl, "dl"), ("e", T.lo, "lo")):
-            if kind in UNITS[t]:
-                dma("sy", "d%s%d" % (kind, t), [(col(buf, 2 * t + 1), col(buf, 2 * t))], ["%s%d" % (key, t)], ["%s2%d" % (key, t)])
+        vop(lambda: ve.tensor_scalar(col(T.dl, t), T.ad[:], 0.5, -1.0, A.max, A.mult), ["ad"], ["dl%d" % t], E // 2, -1)
+        pop(lambda: g.affine_select(col(T.lo, 2 * t + 1), lo, [[0, E]], A.is_ge, 0.0, 0, 0), ["lo%d" % t], ["lo2%d" % t], E, 0)
 
     prep(r)
 
@@ -197,11 +198,10 @@ def build(r, g, T, topo):
         scatter(0)
         dma("sy", "dtc", [(col(T.tic, r, 192), T.ti[r::16, :])], ["ti"], ["tic%d" % r])
         add("po", [], lk_(r, 0) + ["tic%d" % r], ["tic%d" % r], 0, 0)
-        bcast(col(T.tic, r, 192), ["tic%d" % r], "art%d" % r, 768)
-        dma("sy", "dtr", [(T.ti[k::16, :], col(T.tic, k, 192)) for k in others], ["tic%d" % k for k in others], ["ti"], 3000)
-        rows(p16, 17, "p16", pr=1)
-        vop(lambda: ve.tensor_scalar(wm, w0, -2.0 * OFS, None, A.mult), ["w0"], ["wm"], 64)
-        vop(lambda: ve.tensor_scalar(T.none[:], z16, V - OFS - 0.5, None, A.is_ge), [zk], ["none"], 256)
+        bcast(col(T.tic, r, 192), ["tic%d" % r], "art%d" % r, 768, margin=7000)
+        dma("sy", "dtr", [(T.ti[k::16, :], col(T.tic, k, 192)) for k in others], ["tic%d" % k for k in others], ["ti"], 5000)
+        rows(p16, 17, "p16", pr=1, top=V - 0.5)
+        vop(lambda: ve.tensor_scalar(wm, w0, -float(V), None, A.mult), ["w0"], ["wm"], 64)
         mm(T.m1[:], col(T.bm, r, 128), z16, True, True, ["bm%d" % (r // 4), zk], "m1")
         vop(lambda: ve.tensor_tensor(T.eqv[:], z16, T.m1[:], A.is_equal), [zk], ["eqv", "m1"], E)
         vop(lambda: ve.tensor_copy(T.lk[:], T.ti[:, 0:V].indirect(lst(r, 16, 2))), ["ti"] + lk_(r, 16, 2), ["lk"], 2 * G1, 0)
@@ -229,34 +229,30 @@ def build(r, g, T, topo):
 
     def decide(t, ub, uk, bb, bk):
         z, key = (col(T.zc, 1), "zc1") if t == LAST else (z16, zk)
-        for k in others:
+        last = sorted(others, key=lambda k: k == LAST - 1) if t == LAST else others
+        for k in last:
             buf, kk = (T.lanq, "lanq%d" % k) if t == LAST else (T.land, "land%d" % k)
-            turned(T.m1, "m1", buf, k, i15, [kk], False, k == others[-1])
-        vop(lambda: ve.tensor_scalar(T.ok[:], T.m1[:], BIG, BIG, A.add, A.is_equal), [], ["ok", "m1"], E, 0)
-        mm(T.m1[:], gm, T.ok[:], True, True, ["gm", "ok"], "m1", 0)
-        if t == LAST and r < LAST:
-            mm(col(T.pb1, 0), gm4, T.ok[:], True, True, ["gm4", "ok"], "pb1_0", 0)
-        aop(lambda: ac.activation(hit[t][:, 0:E], T.m1[:], F.Sign), [], ["hit%d" % t, "m1"], E, 0)
+            turned(T.m1, "m1", buf, k, i15, [kk], False, k == last[-1])
+        ok, ko = hit[t][:, 0:E], "hit%d" % t
+        vop(lambda: ve.tensor_scalar(ok, T.m1[:], BIG, BIG, A.add, A.is_equal), [], [ko, "m1"], E, 0)
         if t < LAST:
             for to in ([t + 1], [k for k in others if k != t + 1]) if t < LAST - 1 else (others,):
                 bcast(hit[t][:], ["hpad%d" % t, "hit%d" % t], "arh%d" % t, 264 if len(to) == 1 else 1056,
                       margin=LATE[4 + t] + (3000 if len(to) == 3 else 0), ranks=to)
-        elif r < LAST:
-            aop(lambda: ac.activation(hit[5][:, 0:E], col(T.pb1, 0), F.Sign), [], ["hit5", "pb1_0"], E, 0)
-            vop(lambda: ve.tensor_tensor(col(T.fp, 1), hit[LAST][:, 0:E + 16].indirect(col(T.lkl, 2 * LAST + 1, 32)), col(T.fp, 0), A.is_lt),
-                ["hit%d" % LAST, "hpad%d" % LAST, "lkl", "fp0"], ["fp1"], G1, 0)
-            vop(lambda: ve.tensor_tensor(T.flag[:], hit[5][:, 0:E + 16].indirect(col(T.lkl, 2 * LAST, 32)), col(T.fp, 1), A.is_lt),
-                ["hit5", "hpad5", "lkl", "fp1"], ["flag"], G1, 0)
+        if t == r:
+            mm(T.m1[:], gm, ok, True, True, ["gm", ko], "m1", 1 if r == LAST else 0)
+            aop(lambda: ac.activation(T.ok[:], T.m1[:], F.Sign), [], ["ok", "m1"], E, 0)
         mm(ub, T.cm[:, 0:128], T.onesb[:, 0:E], True, False, ["cm0", "ob", "onesb"], uk, 0)
-        mm(ub, um, T.ok[:], False, True, ["um", "ok"], uk, 0)
-        vop(lambda: ve.tensor_tensor(T.mz[:], z, ub, A.min), [key], ["mz", uk], E, 0)
-        mm(bb, T.cm[:, 128:256], T.onesb[:, 0:E], True, False, ["cm1", "ob", "onesb"], bk, 0)
-        mm(bb, wm, T.ok[:], False, False, ["wm", "ok"], bk, 0)
+        mm(ub, um, ok, False, True, ["um", ko], uk, 0)
+        vop(lambda: ve.tensor_tensor(T.mz[:], z, ub, A.min), [key], ["mz", uk], E, 3 if t == LAST > r else 0)
+        if t == r:
+            mm(bb, T.cm[:, 128:256], T.onesb[:, 0:E], True, False, ["cm1", "ob", "onesb"], bk, 0)
+        mm(bb, wm, ok, t != r, False, ["wm", ko], bk, 0)
         mm(bb, gm, T.mz[:], False, True, ["mz"], bk, 0)
         c = int(t == LAST); sp = T.sep[0::16, c * E:(c + 1) * E]
         if t == r == LAST:
             vop(lambda: ve.tensor_tensor(T.eqs[:], z16, bb, A.is_equal), [zk], ["eqs", bk], E, 0)
-        aop(lambda: ac.activation(col(T.sep, c), bb, F.Identity, bias=float(OFS)), [], ["sep%d" % c, bk], E, 0)
+        aop(lambda: ac.activation(col(T.sep, c), bb, F.Identity, bias=float(OFS + (0 if t == r else 264 * 128))), [], ["sep%d" % c, bk], E, 0)
         if t < LAST:
             vop(lambda: ve.tensor_tensor(T.eqs[:], z16, bb, A.is_equal), [zk], ["eqs", bk], E, 0)
             dma("sy", "dsc", [(col(T.sepc, t, 32), sp)], ["sep0"], ["sepc%d" % t])
@@ -274,7 +270,7 @@ def build(r, g, T, topo):
     rounds = []
     for t in range(RO):
         sv = [i for i in range(16) if i != t]; un = []
-        for u in UNITS[t].split():
+        for u in (UNITS[t] if t < LAST else ENDS[r]).split():
             n = int(u[1]); un.append((t, sv[-n:], u[0])); sv = sv[:-n]
         rounds.append(un)
     e0 = EARLY[r]
@@ -283,42 +279,36 @@ def build(r, g, T, topo):
 
     def unit(s):
         t, sl, kind = units[s]; n = len(sl)
-        a = NA + take("s") % NG if kind in "se" else take("a") % NA
-        ab, sa, sb = [buf[:, 1024 * a:1024 * a + E * n] for buf in (T.ab, T.sa, T.sb)]
+        a = NA + take("s") % NG if kind == "s" else take("a") % NA
+        ab, sa = [buf[:, 1024 * a:1024 * a + E * n] for buf in (T.ab, T.sa)]
         ka, ksa, ksb = [["%s%d_%d" % (x, a, j) for j in range(n)] for x in ("ab", "sa", "sb")]
-        lo, dl = col(T.lo, 2 * t), col(T.dl, 2 * t)
-        rv = ["relv"] if s == S - FREE_V else []; ra = ["rela"] if s == S - FREE_A else []
-        if s > e0 + 2 and units[s - 2][0] == int(r == 0) != units[s - 1][0]:
-            ra = ra + ["quiet"]
-        tiles = [(col(sa, j), col(sb, j)) for j in range(n)]
-        if kind in "se":
-            aop(lambda: ac.activation(ab, xw.indirect(lst(t, sl[0], n)), F.Copy, scale=1.0 if kind == "s" else -1.0), XS + lk_(t, sl[0], n), ka, n * G1, GPR)
-        else:
-            for j, i in enumerate(sl):
-                vop(lambda j=j, i=i: ve.tensor_tensor(col(ab, j), xw.indirect(lst(t, i)), lo, A.subtract), XS + ["lo%d" % t] + lk_(t, i), [ka[j]], G1)
+        lo, dl = col(T.lo, 2 * t), col(T.dl, t)
+        rv = ["relv"] if s == S - FREE_V else []
+        ra = (["rela"] if s == S - FREE_A[r] else []) + (["quiet"] if s == QUIET else [])
         if kind == "s":
-            for j in range(n):
-                pb, kb = ring(True); out = col((T.sa, T.sb)[j], a, 1024); tiles[j] = (col(out, 0), col(out, 1))
-                mms([(col(pb, h), nid, lo, True, False) for h in range(2)] + [(col(pb, 1), ident, dl, False, False)], ["id1", "lo%d" % t, "dl%d" % t], kb)
-                mms([(col(pb, h), ident, col(ab, j), False, True) for h in range(2)], ["id0", ka[j]], kb)
-                aop(lambda out=out, pb=pb: ac.activation(out, pb[:], F.Sign), [], [ksa[j], ksb[j]] + kb + ra, 2 * E)
+            aop(lambda: ac.activation(ab, xw.indirect(lst(t, sl[0])), F.Copy), XS + lk_(t, sl[0]), ka, G1)
+            pb, kb = ring(True); out = col(T.sa, a, 1024); tiles = [(col(out, 0), col(out, 1))]
+            mms([(col(pb, h), nid, lo, True, False) for h in range(2)] + [(col(pb, 1), ident, dl, False, False)],
+                ["id1", "lo%d" % t, "dl%d" % t] + (lk_(t, sl[0]) if s == 0 else []), kb)
+            mms([(col(pb, h), ident, ab, False, True) for h in range(2)], ["id0"] + ka, kb)
+            aop(lambda: ac.activation(out, pb[:], F.Sign), [], ksa + ksb + kb + ra, 2 * E)
         else:
-            if kind == "e":
-                add("po", [lambda: g.dma_start(ab, T.lo[:, 1024 * t:1024 * t + E * n], accum_op=A.add)], ["lo%d" % t, "lo2%d" % t], ka, 1000, 0, DLAT, "da%d" % a)
+            sb = T.sb[:, 1024 * a:1024 * a + E * n]; tiles = [(col(sa, j), col(sb, j)) for j in range(n)]
+            if n == 2 and sl[1] == sl[0] + 1 and s >= 2:
+                vop(lambda: ve.tensor_tensor(ab, xw.indirect(lst(t, sl[0], 2)), col(T.lo, t, 1024), A.subtract),
+                    XS + ["lo%d" % t, "lo2%d" % t] + lk_(t, sl[0], 2), ka, 2 * G1)
+            else:
+                for j, i in enumerate(sl):
+                    vop(lambda j=j, i=i: ve.tensor_tensor(col(ab, j), xw.indirect(lst(t, i)), lo, A.subtract), XS + ["lo%d" % t] + lk_(t, i), [ka[j]], G1)
             if kind == "m":
                 aop(lambda: ac.activation(sa, ab, F.Sign), ka, ksa + rv, n * E)
             else:
                 vop(lambda: ve.tensor_scalar(sa, ab, -1.0, 1.0, A.max, A.min), ka, ksa + rv, n * 256)
-            if kind == "d":
-                add("po", [lambda: g.dma_start(ab, T.dl[:, 1024 * t:1024 * t + E * n], accum_op=A.add)], ["dl%d" % t, "dl2%d" % t], ka, 1000, 0, DLAT, "da%d" % a)
-                aop(lambda: ac.activation(sb, ab, F.Sign), ka, ksb + ra, n * E)
-            else:
-                pb, kb = ring(kind == "e")
-                for j in range(n):
-                    mm(col(pb, j), nid if kind == "e" else ident, dl, True, False, ["id0", "id1", "dl%d" % t], kb[j])
-                    mm(col(pb, j), ident, col(ab, j), False, True, [ka[j]], kb[j])
-                aop(lambda: ac.activation(sb, pb[:, 0:E * n], F.Sign), [], ksb + kb[:n] + ra, n * E)
-        wa, wb = (gm, ngm) if kind == "e" else (ngm, gm)
+            pb, kb = ring()
+            for j in range(n):
+                mm(col(pb, j), ident, dl, True, False, ["id0", "dl%d" % t], kb[j])
+                mm(col(pb, j), ident, col(ab, j), False, True, [ka[j]], kb[j])
+            aop(lambda: ac.activation(sb, pb[:, 0:E * n], F.Sign), [], ksb + kb[:n] + ra, n * E)
         one = t == r and r and s >= e0
         fin = s + 1 == S or units[s + 1][0] != t or s + 1 == e0
         if one and (s == e0 or units[s - 1][0] != t):
@@ -332,8 +322,8 @@ def build(r, g, T, topo):
         for j, i in enumerate(sl):
             for blk in range(4):
                 o = T.red[:, 128 * blk + i:128 * blk + 128:16]
-                it += [(o, col(tiles[j][0], blk, 128), wa[:, 0::16], not one, False),
-                       (o, col(tiles[j][1], blk, 128), wb[:, 0::16], False, not one or (fin and j == n - 1 and blk == 3))]
+                it += [(o, col(tiles[j][0], blk, 128), ngm[:, 0::16], not one, False),
+                       (o, col(tiles[j][1], blk, 128), gm[:, 0::16], False, not one or (fin and j == n - 1 and blk == 3))]
         if one and fin:
             mms(it, ksa + ksb + ["gm", "ngm"], ["red"])
         else:
@@ -378,26 +368,24 @@ def build(r, g, T, topo):
     turned(T.m1, "m1", T.part, LAST, i15, ["id2", "part%d" % LAST], True)
     mm(T.m1[:], col(T.dm, LAST - 1, 128), rm4, False, False, ["dm", rmk], "m1", 0)
     todo = list(range(RO + ahead, 16)) + [i for i in range(LAST) if i != r]
-    mm(fb, n256i, T.none[:], True, False, ["id3", "none", "relv"], fk, 2)
+    if r < LAST:
+        mm(fb, hw, T.ok[:], True, False, ["hw", "ok", "relv"], fk, 2)
+    else:
+        mm(fb, ident, col(T.eq, RO), True, False, ["eq%d" % RO, "relv"], fk, 2)
 
-    def acc(w, x, R, stop=False):
-        mms([(fb, w, x, False, stop)], R + ([] if stop else [fk]), [fk] if stop else [], 2)
-
-    def f_own():
-        acc(p128i, hit[r][:, 0:E], ["id4", "hit%d" % r])
-        acc(n256i, T.eqs[:], ["eqs"], r == LAST)
+    def acc(w, x, R, stop=False, pr=2):
+        mms([(fb, w, x, False, stop)], R + ([] if stop else [fk]), [fk] if stop else [], pr)
 
     def differ(i, n):
         bank, key = banks[n % 2] if n < M3 else banks[n % 3]
-        mms([(bank, md, col(T.zall, i), True, i >= LAST)] + ([(bank, p32i, col(T.rem, 2 * i + 1), False, True)] if i < LAST else []),
-            ["md", "zall", "id5", "relv"] + (["rem%d" % (2 * i + 1)] if i < LAST else []), [key])
+        mms([(bank, md, col(T.zall, i), True, i >= LAST)] + ([(bank, g32, col(T.rem, 2 * i + 1), False, True)] if i < LAST else []),
+            ["md", "zall", "id6", "relv"] + (["rem%d" % (2 * i + 1)] if i < LAST else []), [key])
         return bank, key
 
-    acc(n256i, T.eqv[:], ["eqv"])
-    for i in range(RO, RO + ahead):
-        acc(p2i, col(T.eq, i), ["id6", "eq%d" % i])
+    for i in range(RO + 1, RO + ahead):
+        acc(ident, col(T.eq, i), ["eq%d" % i])
     if r < LAST:
-        f_own()
+        acc(n256i, T.eqs[:], ["id3", "eqs"])
         bank4, key4 = differ(LAST, 1)
         vop(lambda: ve.tensor_scalar(col(T.eq, LAST), bank4, 0.0, None, A.is_equal), [], ["eq%d" % LAST, key4], E, 2)
         acc(ident, col(T.eq, LAST), ["eq%d" % LAST])
@@ -412,13 +400,18 @@ def build(r, g, T, topo):
     for n in (len(todo) - 2, len(todo) - 1):
         c = n % 4
         vop(lambda c=c: ve.tensor_scalar(col(T.eq, c ^ 2), col(T.eq, c), 0.0, None, A.is_equal), ["eq%d" % c], ["eq%d" % (c ^ 2)], E // 2, 2)
-        acc(p2i, col(T.eq, c ^ 2), ["id6", "eq%d" % (c ^ 2)], r < LAST and n == len(todo) - 1)
-    if r < LAST:
-        aop(lambda: ac.activation(col(T.fp, 0), fb, F.Identity, bias=-128.0), [], ["fp0", fk], E, 0)
+        acc(p32i, col(T.eq, c ^ 2), ["id5", "eq%d" % (c ^ 2)])
     decide(LAST, col(T.pb0, 1), "pb0_1", T.red[:], "red")
     if r == LAST:
-        f_own()
-        vop(lambda: ve.tensor_scalar(T.flag[:], fb, 128.5, None, A.is_gt), [], ["flag", fk], E, 0)
+        acc(hw, T.ok[:], ["hw", "ok"], False, 0)
+        acc(n256i, T.eqs[:], ["id3", "eqs"], True, 0)
+    else:
+        rem(LAST, 0)
+        vop(lambda: ve.tensor_copy(col(T.eq, RO), hit[LAST][:, 0:E + 16].indirect(col(T.lkl, 2 * LAST + 1, 32))),
+            ["hit%d" % LAST, "hpad%d" % LAST, "lkl"], ["eq%d" % RO], G1, -1)
+        acc(col(T.dm, LAST, 128), col(T.rem, 2 * LAST), ["dm", "rem%d" % (2 * LAST)], False, 0)
+        acc(ngm, col(T.eq, RO), ["ngm", "eq%d" % RO], True, 0)
+    vop(lambda: ve.tensor_scalar(T.flag[:], fb, 128.5, None, A.is_gt), [], ["flag", fk], E, -1)
     dma("sy", "dfl", [(T.yflag[:], T.flag[:])], ["flag"], [])
     for k in range(LAST):
         if k != r:
@@ -429,6 +422,7 @@ def build(r, g, T, topo):
 def order(ranks):
     ext = {}
     for ops in ranks:
+        next(o for o in ops if o["sends"])["cost"] += 2500
         for o in ops:
             o["next"] = []
             for k, keys, sem, n in o["sends"]:
@@ -457,28 +451,22 @@ def order(ranks):
             cand.setdefault((r, o["q"]), [])
             if not pre:
                 cand[(r, o["q"])].append(o)
-    free = {q: 0.0 for q in cand}; out = [[] for _ in ranks]; called = set()
+    free = {q: 0.0 for q in cand}; out = [[] for _ in ranks]; pick = {}
     while True:
-        best = None
         for q, c in cand.items():
-            if c:
+            if q not in pick and c:
                 t0 = max(free[q], min(o["ready"] for o in c))
                 o = min((o for o in c if o["ready"] <= t0 + (SLACK if o["pr"] > 0 else URGENT)), key=lambda o: o["key"])
-                t = max(t0, o["ready"])
-                if best is None or t < best[0]:
-                    best = (t, q, o)
-        if best is None:
+                pick[q] = (max(t0, o["ready"]), o)
+        if not pick:
             return out
-        t, q, o = best
-        cand[q].remove(o); out[q[0]].append(o)
-        free[q] = t + o["cost"] + (2500 if o["sends"] and q not in called else 0)
-        if o["sends"]:
-            called.add(q)
+        q = min(pick, key=lambda q: pick[q][0]); t, o = pick.pop(q)
+        cand[q].remove(o); out[q[0]].append(o); free[q] = t + o["cost"]
         for x in o["next"]:
             x["ready"] = max(x["ready"], free[q] + (0 if q == (x["r"], "pe") and x["q"] == "pe" else o["lat"] + HOP))
             x["left"] -= 1
             if x["left"] == 0:
-                cand[(x["r"], x["q"])].append(x)
+                cand[(x["r"], x["q"])].append(x); pick.pop((x["r"], x["q"]), None)
 
 
 def rank_program(g, core, T, topo):

from concourse.bass import DstId, RemoteDMATransfer
from concourse.mybir import AluOpType as A, ActivationFunctionType as F

V, E, RO, N = 3072, 512, 5, 5
LAST = RO - 1
LW = 18 * 32
OFS = 2048
BIG = 1.5 * 2 ** 28
NA, NG = 4, 2
UNITS = ["s1 v2 v2 s1 v2 m2 v2 s1 v2", "s1 v2 m2 v2 s1 v2 m2 v2 v1", "s1 v2 v2 m2 s1 v2 v2 m2 v1", "s1 v2 m2 v2 s1 v2 m2 v2 v1"]
ENDS = ["s1 v2 s1 v2 v2 v2 v2 v2 v1"] + ["s1 v2 v2 v2 v2 v2 v2 v2"] * 3 + ["s1 v2 s1 v2 v2 v2 v2 v2 v1"]
EARLY = [0, 4, 4, 4, 2]
EQ4 = 6
QUIET = 13
PREP = 6
FREE_V, FREE_A = 2, [2, 6, 6, 6, 8]
M3, REDP = 2, 1.3
CY, PC, GA, SC, HOP, SLACK, URGENT, MARGIN = 0.87, 0.46, 1.6, 3.5, 120, 100, 150, 2000
LATE = (7000, 4500, 2500, 1000, 3500, 2500, 1000, 800)
BF, F16, F32 = "bfloat16", "float16", "float32"
SB = {"adjs": (V, "int32"), "adj0": (V, "int32"), "xs": (V + 16, BF), "tvs": (160, "int32"), "vl": (160, "uint16"),
      "ti": (V, F32), "tic": (5 * 192, F32), "io2": (E, F32), "onesb": (V // 2, BF), "n256": (128, BF), "sw": (E, BF),
      "idm": (9 * 128, BF), "gm": (9 * 128, BF), "cm": (256, BF), "dm": (640, BF), "bm": (2048, BF),
      "py": (E, F16), "pc": (E, F16), "pt": (E, F16), "zc": (2 * E, F16), "zt": (E, F16), "zall": (16 * E, F16),
      "off": (5 * LW, "uint16"), "eqv": (E, BF), "lk": (1024, F16), "lt": (1024, F16),
      "lkl": (320, "uint16"), "rem": (9 * E, BF), "lk4": (32, "uint16"), "rm4": (E, BF),
      "xv": (5 * E, BF), "xy": (2 * E, BF), "ad": (E, BF), "lo": (10 * E, BF), "dl": (5 * E, BF),
      "ab": ((NA + NG) * 1024, BF), "sa": ((NA + NG) * 1024, BF), "sb": (NA * 1024, BF),
      "part": (6 * E, BF), "land": (5 * E, BF), "lanq": (5 * E, BF), "ok": (E, BF), "mz": (E, F16),
      "sep": (2 * E, F32), "sepc": (5 * 32, F32), "eqs": (E, BF), "eq": (16 * E, BF), "flag": (E, BF)}
SB.update({"hit%d" % k: (E + 16, BF) for k in range(5)})
SCRATCH = {k: ("sbuf", [128, w], d) for k, (w, d) in SB.items()}
SCRATCH.update({k: ("psum", [128, w], F32) for k, w in (("pb0", 1024), ("pb1", 1024), ("pb2", 1024), ("red", E), ("m1", E))})
SEMAPHORES = (["ve", "ac", "pe", "po", "ls", "arp", "arz", "ark", "arw6", "arw12", "dtv", "dadj", "dadj0", "dx", "dtc", "dtr", "dsc", "dfl"]
              + ["%s%d" % (a, k) for a in ("do", "dz", "ary", "arl", "art", "arh", "ars", "arq") for k in range(5)])
PLAN = []


def build(r, g, T, topo):
    core = T.cores[r]; ops = []
    ve, ac, pe = g.vector, g.scalar, g.tensor
    others = [k for k in range(N) if k != r]

    def add(q, fns, R, W, cost, pr=1, lat=0, sem=None, sends=()):
        ops.append(dict(q=q, fns=fns, R=list(R), W=list(W), cost=cost, pr=pr, lat=lat, sem=sem, sends=sends, r=r))

    def vop(fn, R, W, n, pr=1):
        add("ve", [fn], R, W, 50 + max(64, n) * CY, pr)

    def aop(fn, R, W, n, pr=1):
        add("ac", [fn], R, W, 65 + max(64, n) * CY, pr)

    def pop(fn, R, W, n, pr=1):
        add("po", [fn], R, W, 170 + 2 * n * CY, pr)

    def mms(items, R, W, pr=1):
        add("pe", [lambda m=m: pe.matmul(*m) for m in items], R, W, sum(PC * max(64, m[2].shape[1]) for m in items), pr)

    def mm(out, lhsT, rhs, start, stop, R, bank, pr=1):
        mms([(out, lhsT, rhs, start, stop)], R, [bank], pr)

    def dma(q, sem, items, R, W, lat=2000, pr=0):
        Q = g.sync if q == "sy" else ac
        add(q, [lambda m=m: Q.dma_start(*m) for m in items], R, W, 60 * len(items), pr, lat, sem)

    def dst(k):
        rid, pid, se = topo.addr(T.cores[k])
        return DstId(rid=rid, pnc=pid)

    def bcast(ap, keys, sem, nbytes, to=None, tkeys=None, margin=MARGIN, ranks=others):
        el = [topo.engines(core, T.cores[k])[n::1 if len(ranks) == 1 else len(others)] for n, k in enumerate(ranks)]
        tr = [RemoteDMATransfer(dst_ids=[dst(k)], dma_engine_mask=sum(1 << e for e in el[n]), remote_sem=T.sem[sem], src=ap,
                                dst=ap if to is None else to) for n, k in enumerate(ranks)]
        add("po", [lambda: g.remote_dma_fused(tr, local_sem=T.sem.ls)], keys, [], 700, 0, 1600 + 1.5 * nbytes + margin, "ls",
            [(k, tkeys or keys, sem, len(el[n])) for n, k in enumerate(ranks)])

    col = lambda buf, k, w=E: buf[:, k * w:(k + 1) * w]
    lst = lambda t, i, n=1: T.off[:, t * LW + 32 * i:t * LW + 32 * (i + n)]
    lk_ = lambda t, i, n=1: ["off%d_%d" % (t, j) for j in range(i, i + n)]
    xw, aw, ob = T.xs[:, 0:V + 16], T.adjs[:, 0:V], T.onesb[:, 0:128]
    ident, nid, i15, n256i, p128i, p32i, g32, nsi, md = [col(T.idm, k, 128) for k in range(9)]
    g0, gm, ngm, um, wm, hw, w0, u0, w1 = [col(T.gm, k, 128) for k in range(9)]
    hit = [T["hit%d" % k] for k in range(5)]
    z16, p16, zk = col(T.zc, int(r == LAST)), T.pc[:], "zc%d" % int(r == LAST)
    G1 = GA * E; XS = ["xs", "xpad"]

    dma("ac", "dtv", [(T.tvs[:], T.tv[:])], [], ["tvs"], 1800)
    dma("sy", "dx", [(T.xs[:, 0:V], T.x[:])], [], ["xs"], 3600)
    vop(lambda: ve.memset(ob, 1.0), [], ["ob"], 64)
    vop(lambda: ve.memset(T.onesb[:, 128:V // 2], 1.0), [], ["onesb"], 704)
    vop(lambda: ve.memset(T.adj0[:, 0:2048], 0), [], ["adja"], 2048)
    pop(lambda: g.iota(T.adj0[:, 2048:V], [[0, 1024]], 0, 0), [], ["adjb"], 1024)
    dma("sy", "dadj0", [(T.adj0[r::16, :], T.adj[r::16, :])], ["adja", "adjb"], ["adj0"], 1800)
    dma("sy", "dadj", [(T.adjs[:], T.adj[:])], ["adja", "adjb"], ["adjs"], 6200)

    def const(out, src, R, key, scale):
        aop(lambda: ac.activation(out, src, F.Identity, scale=float(scale)), R, [key], out.shape[1])

    for h in range(2):
        const(col(T.ti, h, V // 2), T.onesb[:], ["ob", "onesb"], "ti", E)
    pop(lambda: g.iota(T.io2[:], [[1, E]], 0, 0, allow_small_or_imprecise_dtypes=True), [], ["io2"], E)
    for n in range(4):
        pop(lambda n=n: g.affine_select(col(T.sw, n, 128), ob, [[-32, 4], [128, 2], [-1, 16]], A.is_equal, 0.0, -16 * (n // 2) - 128 * (n % 2), 1),
            ["ob"], ["sw%d" % n], 128)
    pop(lambda: g.affine_select(ident, ob, [[-1, 128]], A.is_equal, 0.0, 0, 1), ["ob"], ["id0"], 128)

    def ingroup(out, src, key, okey):
        pop(lambda: g.affine_select(g0, src, [[-16, 8], [0, 16]], A.is_ge, 0.0, 0, 1), [key], ["g0"], 128)
        pop(lambda: g.affine_select(out, g0, [[16, 8], [0, 16]], A.is_ge, 0.0, 15, -1), ["g0"], [okey], 128)

    ingroup(gm, ob, "ob", "gm")
    vop(lambda: ve.tensor_copy(T.vl[:], T.tvs[:]), ["tvs"], ["vl"], 160, 0)
    vop(lambda: ve.tensor_copy(lst(r, 17), T.tvs[:, 32 * r:32 * r + 32]), ["tvs"], lk_(r, 17), 64, 0)
    vop(lambda: ve.memset(T.xs[:, V:V + 16], 300.0), [], ["xpad"], 64)
    vop(lambda: ve.memset(T.red[:], 0.0), [], ["red"], E)
    vop(lambda: ve.memset(T.cm[:, 0:128], -16.0), [], ["cm0"], 64)
    vop(lambda: ve.memset(T.cm[:, 128:256], 264.0), [], ["cm1"], 64)
    for k in sorted({r, LAST}):
        vop(lambda k=k: ve.memset(hit[k][:, E:E + 16], 0.0), [], ["hpad%d" % k], 64)

    def scatter(h):
        vop(lambda: ve.tensor_copy(T.ti[:, 0:V].indirect(lst(r, 16 + h)), T.io2[:]), ["io2"] + lk_(r, 16 + h), ["ti"], SC * E)

    scatter(1)
    for t0, n in ((r, 1), (0, r), (r + 1, LAST - r)):
        if n:
            aop(lambda t0=t0, n=n: ac.activation(T.xv[:, t0 * E:(t0 + n) * E], xw.indirect(T.vl[:, 32 * t0:32 * (t0 + n)]), F.Copy),
                XS + ["vl"], ["xv%d" % t for t in range(t0, t0 + n)], n * G1, 0 if t0 == r else 1)
    for k, c in ((0, -1), (1, 1.5), (2, -256), (3, 128), (4, 32), (6, -1 / 256)):
        const(col(T.idm, k + 1, 128), ident, ["id0"], "id%d" % (k + 1), c)
    const(ngm, gm, ["gm"], "ngm", -1)
    const(u0, gm, ["gm"], "u0", -V)
    const(T.n256[:], gm, ["gm"], "n256", -256)
    const(g32, gm, ["gm"], "id6", 32)
    for c in ((0,), (1, 2))[r == LAST]:
        pop(lambda c=c: g.affine_select(col(T.bm, c), T.onesb[:, 0:E], [[-1, 4], [-16, 8], [0, 16]], A.is_equal, 0.0, -4 * c, 1),
            ["ob", "onesb"], ["bm%d" % c], E)

    def rows(dstb, i, key, win=aw, wk="adjs", pr=0, top=V):
        vop(lambda: ve.tensor_scalar(dstb, win.indirect(lst(r, i)), -float(OFS), float(top - OFS), A.add, A.min), [wk] + lk_(r, i), [key], G1, pr)

    def swap(bank, c0, src, i, n, key, bkey):
        mms([(bank[:, c0 + q:c0 + 2 * n:2], col(T.sw, 2 * q + gl, 128), src[:, 16 * gl + i::32], gl == 0, gl == 1) for q in range(2) for gl in range(2)],
            ["sw0", "sw1", "sw2", "sw3", key], [bkey], 0)

    def turn(dstb, src, key, dkey, n=E):
        vop(lambda: ve.transpose(dstb, src), [key], [dkey], n // 2, 0)

    def tolist(i, n, bank, bkey):
        vop(lambda: ve.tensor_scalar(lst(r, i, n), bank, float(OFS), None, A.add), [], lk_(r, i, n) + [bkey], 32 * n, 0)

    rows(T.py[:], 17, "py", T.adj0[:, 0:V], "adj0"); turn(T.pt[:], T.py[:], "py", "pt"); swap(T.m1, 0, T.pt, r, 16, "pt", "m1")
    tolist(16, 1, T.m1[:, 0:32], "m1")
    bcast(lst(r, 16), lk_(r, 16), "ary%d" % r, 64, margin=0)
    rows(z16, 16, zk); turn(T.zt[:], z16, zk, "zt")
    for i0, n, bank, key in ((12, 4, T.m1, "m1"), (6, 6, T.pb1, "pb1_0"), (0, 6, T.m1, "m1")):
        for i in range(i0, i0 + n):
            swap(bank, 32 * i, T.zt, i, 16, "zt", key)
        tolist(i0, n, bank[:, 32 * i0:32 * (i0 + n)], key)
        if r == 0:
            bcast(lst(0, i0, n), lk_(0, i0, n), "arl0" if i0 == 0 else "arw%d" % i0, 64 * n, margin=2500)
    if r:
        bcast(lst(r, 0, 16), lk_(r, 0, 16), "arl%d" % r, 1024)
    if r == LAST:
        bcast(z16, [zk], "arz", 1024)
    pop(lambda: g.affine_select(um, u0, [[1, 128]], A.is_gt, 0.0, 0, -1), ["u0"], ["um"], 128)
    pop(lambda: g.affine_select(um, um, [[-1, 128]], A.not_equal, float(V), 0, 1), [], ["um"], 128)
    for k in range(RO):
        pop(lambda k=k: g.affine_select(col(T.dm, k, 128), T.n256[:], [[0, 8], [1, 16]], A.is_equal, 0.0, -k, 0), ["n256"], ["dm"], 128)
    pop(lambda: g.iota(w0, [[-16, 8], [0, 16]], -14, 1, allow_small_or_imprecise_dtypes=True), [], ["w0"], 128)
    ingroup(w0, w0, "w0", "w0")
    pop(lambda: g.affine_select(hw, p128i, [[-16, 8], [0, 16]], A.not_equal, 0.0, -r, 1), ["id4"], ["hw"], 128)

    seen = {"a": 0, "p": 0, "s": 0}

    def take(key):
        seen[key] += 1
        return seen[key] - 1

    def ring(side=False):
        p = 2 if side else take("p") % 2
        return T["pb%d" % p], ["pb%d_0" % p, "pb%d_1" % p]

    def prep(t):
        xv, xy, kv, ky = col(T.xv, t), col(T.xy, t % 2), "xv%d" % t, "xy%d" % (t % 2)
        aop(lambda: ac.activation(xy, xw.indirect(lst(t, 16)), F.Copy), XS + lk_(t, 16), [ky], G1, 1 if t and t != r else 0)
        pb, kb = ring(True); lo = col(T.lo, 2 * t)
        mm(col(pb, 0), ident, xv, True, True, ["id0", kv], kb[0], -1)
        mms([(col(pb, 1), ident, xv, True, False), (col(pb, 1), nid, xy, False, True)], ["id1", kv, ky], [kb[1]], -1)
        vop(lambda: ve.tensor_tensor(lo, xy, col(pb, 0), A.min), [ky], ["lo%d" % t, kb[0]], E, -1)
        aop(lambda: ac.activation(T.ad[:], col(pb, 1), F.Abs), [], ["ad", kb[1]], E, -1)
        vop(lambda: ve.tensor_scalar(col(T.dl, t), T.ad[:], 0.5, -1.0, A.max, A.mult), ["ad"], ["dl%d" % t], E // 2, -1)
        pop(lambda: g.affine_select(col(T.lo, 2 * t + 1), lo, [[0, E]], A.is_ge, 0.0, 0, 0), ["lo%d" % t], ["lo2%d" % t], E, 0)

    prep(r)

    def links():
        scatter(0)
        dma("sy", "dtc", [(col(T.tic, r, 192), T.ti[r::16, :])], ["ti"], ["tic%d" % r])
        add("po", [], lk_(r, 0) + ["tic%d" % r], ["tic%d" % r], 0, 0)
        bcast(col(T.tic, r, 192), ["tic%d" % r], "art%d" % r, 768, margin=7000)
        dma("sy", "dtr", [(T.ti[k::16, :], col(T.tic, k, 192)) for k in others], ["tic%d" % k for k in others], ["ti"], 5000)
        rows(p16, 17, "p16", pr=1, top=V - 0.5)
        vop(lambda: ve.tensor_scalar(wm, w0, -float(V), None, A.mult), ["w0"], ["wm"], 64)
        mm(T.m1[:], col(T.bm, r, 128), z16, True, True, ["bm%d" % (r // 4), zk], "m1")
        vop(lambda: ve.tensor_tensor(T.eqv[:], z16, T.m1[:], A.is_equal), [zk], ["eqv", "m1"], E)
        vop(lambda: ve.tensor_copy(T.lk[:], T.ti[:, 0:V].indirect(lst(r, 16, 2))), ["ti"] + lk_(r, 16, 2), ["lk"], 2 * G1, 0)
        turn(T.lt[:], T.lk[:], "lk", "lt", 1024)
        for k in range(RO):
            swap(T.m1, 64 * k, T.lt, k, 32, "lt", "m1")
        vop(lambda: ve.tensor_copy(T.lkl[:], T.m1[:, 0:320]), [], ["lkl", "m1"], 320, 0)
        if r == LAST:
            bcast(col(T.lkl, 2 * LAST - 2, 32), ["lkl"], "ark", 64, T.lk4[:], ["lk4"])
        const(w1, col(T.bm, r, 128), ["bm%d" % (r // 4)], "w1", 1 / 256)
        vop(lambda: ve.tensor_tensor(md, w1, nsi, A.add), ["w1", "id7"], ["md"], 256)

    def copies():
        dma("sy", "dz0", [(col(T.zall, n), z16) for n in range(4)], [zk, "quiet"], ["zall"], 4000, 1)
        dma("sy", "dz1", [(col(T.zall, n, 4 * E), col(T.zall, 0, 4 * E)) for n in range(1, 4)], [], ["zall"], 6000, 1)
        dma("sy", "dz2", [(T.zall[r::16, :], p16)], ["p16"], ["zall"], 2500, 1)

    def rem(k, side, n=1, pr=0, R=()):
        j = 2 * k + side
        aop(lambda: ac.activation(T.rem[:, j * E:(j + n) * E], hit[k][:, 0:E + 16].indirect(T.lkl[:, 32 * j:32 * (j + n)]), F.Copy),
            ["hit%d" % k, "hpad%d" % k, "lkl"] + list(R), ["rem%d" % (j + d) for d in range(n)], n * G1, pr)

    def turned(bank, key, buf, c, w, R, start=False, stop=False):
        mms([(col(bank, b, 128), buf[:, c * E + 128 * b:c * E + 128 * b + 128], w, start and b == 0, stop and b == 3) for b in range(4)], R, [key], 0)

    def decide(t, ub, uk, bb, bk):
        z, key = (col(T.zc, 1), "zc1") if t == LAST else (z16, zk)
        last = sorted(others, key=lambda k: k == LAST - 1) if t == LAST else others
        for k in last:
            buf, kk = (T.lanq, "lanq%d" % k) if t == LAST else (T.land, "land%d" % k)
            turned(T.m1, "m1", buf, k, i15, [kk], False, k == last[-1])
        ok, ko = hit[t][:, 0:E], "hit%d" % t
        vop(lambda: ve.tensor_scalar(ok, T.m1[:], BIG, BIG, A.add, A.is_equal), [], [ko, "m1"], E, 0)
        if t < LAST:
            for to in ([t + 1], [k for k in others if k != t + 1]) if t < LAST - 1 else (others,):
                bcast(hit[t][:], ["hpad%d" % t, "hit%d" % t], "arh%d" % t, 264 if len(to) == 1 else 1056,
                      margin=LATE[4 + t] + (3000 if len(to) == 3 else 0), ranks=to)
        if t == r:
            mm(T.m1[:], gm, ok, True, True, ["gm", ko], "m1", 1 if r == LAST else 0)
            aop(lambda: ac.activation(T.ok[:], T.m1[:], F.Sign), [], ["ok", "m1"], E, 0)
        mm(ub, T.cm[:, 0:128], T.onesb[:, 0:E], True, False, ["cm0", "ob", "onesb"], uk, 0)
        mm(ub, um, ok, False, True, ["um", ko], uk, 0)
        vop(lambda: ve.tensor_tensor(T.mz[:], z, ub, A.min), [key], ["mz", uk], E, 3 if t == LAST > r else 0)
        if t == r:
            mm(bb, T.cm[:, 128:256], T.onesb[:, 0:E], True, False, ["cm1", "ob", "onesb"], bk, 0)
        mm(bb, wm, ok, t != r, False, ["wm", ko], bk, 0)
        mm(bb, gm, T.mz[:], False, True, ["mz"], bk, 0)
        c = int(t == LAST); sp = T.sep[0::16, c * E:(c + 1) * E]
        if t == r == LAST:
            vop(lambda: ve.tensor_tensor(T.eqs[:], z16, bb, A.is_equal), [zk], ["eqs", bk], E, 0)
        aop(lambda: ac.activation(col(T.sep, c), bb, F.Identity, bias=float(OFS + (0 if t == r else 264 * 128))), [], ["sep%d" % c, bk], E, 0)
        if t < LAST:
            vop(lambda: ve.tensor_tensor(T.eqs[:], z16, bb, A.is_equal), [zk], ["eqs", bk], E, 0)
            dma("sy", "dsc", [(col(T.sepc, t, 32), sp)], ["sep0"], ["sepc%d" % t])
            bcast(col(T.sepc, t, 32), ["sepc%d" % t], "ars%d" % t, 128)
        dma("ac" if c else "sy", "do%d" % t, [(T.ysep[:, t * E:(t + 1) * E], sp)], ["sep%d" % c], [])

    def own():
        mm(T.m1[:], n256i, T.eqv[:], True, False, ["id3", "eqv"], "m1", 0)
        turned(T.m1, "m1", T.part, r, i15, ["id2", "part%d" % r])
        for k in range(r):
            rem(k, 0)
            mm(T.m1[:], col(T.dm, k, 128), col(T.rem, 2 * k), False, False, ["dm", "rem%d" % (2 * k)], "m1", 0)
        decide(r, T.m1[:], "m1", T.m1[:], "m1")

    rounds = []
    for t in range(RO):
        sv = [i for i in range(16) if i != t]; un = []
        for u in (UNITS[t] if t < LAST else ENDS[r]).split():
            n = int(u[1]); un.append((t, sv[-n:], u[0])); sv = sv[:-n]
        rounds.append(un)
    e0 = EARLY[r]
    units = rounds[r][:e0] + [u for t in range(RO) for u in (rounds[t][e0:] if t == r else rounds[t])]
    S = len(units)

    def unit(s):
        t, sl, kind = units[s]; n = len(sl)
        a = NA + take("s") % NG if kind == "s" else take("a") % NA
        ab, sa = [buf[:, 1024 * a:1024 * a + E * n] for buf in (T.ab, T.sa)]
        ka, ksa, ksb = [["%s%d_%d" % (x, a, j) for j in range(n)] for x in ("ab", "sa", "sb")]
        lo, dl = col(T.lo, 2 * t), col(T.dl, t)
        rv = ["relv"] if s == S - FREE_V else []
        ra = (["rela"] if s == S - FREE_A[r] else []) + (["quiet"] if s == QUIET else [])
        if kind == "s":
            aop(lambda: ac.activation(ab, xw.indirect(lst(t, sl[0])), F.Copy), XS + lk_(t, sl[0]), ka, G1)
            pb, kb = ring(True); out = col(T.sa, a, 1024); tiles = [(col(out, 0), col(out, 1))]
            mms([(col(pb, h), nid, lo, True, False) for h in range(2)] + [(col(pb, 1), ident, dl, False, False)],
                ["id1", "lo%d" % t, "dl%d" % t] + (lk_(t, sl[0]) if s == 0 else []), kb)
            mms([(col(pb, h), ident, ab, False, True) for h in range(2)], ["id0"] + ka, kb)
            aop(lambda: ac.activation(out, pb[:], F.Sign), [], ksa + ksb + kb + ra, 2 * E)
        else:
            sb = T.sb[:, 1024 * a:1024 * a + E * n]; tiles = [(col(sa, j), col(sb, j)) for j in range(n)]
            if n == 2 and sl[1] == sl[0] + 1 and s >= 2:
                vop(lambda: ve.tensor_tensor(ab, xw.indirect(lst(t, sl[0], 2)), col(T.lo, t, 1024), A.subtract),
                    XS + ["lo%d" % t, "lo2%d" % t] + lk_(t, sl[0], 2), ka, 2 * G1)
            else:
                for j, i in enumerate(sl):
                    vop(lambda j=j, i=i: ve.tensor_tensor(col(ab, j), xw.indirect(lst(t, i)), lo, A.subtract), XS + ["lo%d" % t] + lk_(t, i), [ka[j]], G1)
            if kind == "m":
                aop(lambda: ac.activation(sa, ab, F.Sign), ka, ksa + rv, n * E)
            else:
                vop(lambda: ve.tensor_scalar(sa, ab, -1.0, 1.0, A.max, A.min), ka, ksa + rv, n * 256)
            pb, kb = ring()
            for j in range(n):
                mm(col(pb, j), ident, dl, True, False, ["id0", "dl%d" % t], kb[j])
                mm(col(pb, j), ident, col(ab, j), False, True, [ka[j]], kb[j])
            aop(lambda: ac.activation(sb, pb[:, 0:E * n], F.Sign), [], ksb + kb[:n] + ra, n * E)
        one = t == r and r and s >= e0
        fin = s + 1 == S or units[s + 1][0] != t or s + 1 == e0
        if one and (s == e0 or units[s - 1][0] != t):
            mm(T.red[:], ident, col(T.part, 5), True, False, ["part5"], "red")
        if one and fin and r == LAST:
            turned(T.red, "red", T.eqv, 0, n256i, ["eqv", "id3"])
            for k in range(LAST - 1):
                rem(k, 0)
                turned(T.red, "red", T.rem, 2 * k, col(T.dm, k, 128), ["dm", "rem%d" % (2 * k)])
        it = []
        for j, i in enumerate(sl):
            for blk in range(4):
                o = T.red[:, 128 * blk + i:128 * blk + 128:16]
                it += [(o, col(tiles[j][0], blk, 128), ngm[:, 0::16], not one, False),
                       (o, col(tiles[j][1], blk, 128), gm[:, 0::16], False, not one or (fin and j == n - 1 and blk == 3))]
        if one and fin:
            mms(it, ksa + ksb + ["gm", "ngm"], ["red"])
        else:
            mms(it, ksa + ksb + ["gm", "ngm", "red"], [], REDP)
        if fin:
            c = 5 if s < e0 else t
            aop(lambda: ac.activation(col(T.part, c), T.red[:], F.Identity, bias=16.0 * (c < 5)), [], ["part%d" % c, "red"], E, 0)
            if c == LAST:
                bcast(col(T.part, LAST), ["part%d" % LAST], "arq%d" % r, 1024, col(T.lanq, r), ["lanq%d" % r], 0)
            elif c == r:
                own()
            elif c < LAST:
                bcast(col(T.part, t), ["part%d" % t], "arp", 0, col(T.land, r), ["land%d" % r], LATE[t], [t])

    ahead = EQ4 if r == LAST else 0
    made = {r}
    for s in range(S):
        t = units[min(s + PREP, S - 1)][0]
        if t not in made and (s >= 1 or not r):
            made.add(t); prep(t)
        if s == 0:
            links()
        if s == 1:
            for i in range(RO, RO + ahead):
                bank, key = col(T.pb1, i % 2), "pb1_%d" % (i % 2)
                mm(bank, col(T.bm, i, 128), p16, True, True, ["bm%d" % (i // 4), "p16"], key)
                vop(lambda i=i, bank=bank: ve.tensor_tensor(col(T.eq, i), z16, bank, A.is_equal), [zk], ["eq%d" % i, key], E)
        unit(s)
    copies()

    fb, fk = col(T.pb0, 0), "pb0_0"
    banks = [(col(T.pb2, 0), "pb2_0"), (col(T.pb2, 1), "pb2_1"), (col(T.pb1, 1), "pb1_1")]
    for k in range(LAST):
        if k != r:
            both = k > r or k == LAST - 1
            rem(k, 0 if both else 1, 2 if both else 1, 2, ["rela"])
    rm4, rmk = col(T.rem, 2 * LAST - 2), "rem%d" % (2 * LAST - 2)
    if r < LAST:
        rm4, rmk = T.rm4[:], "rm4"
        aop(lambda: ac.activation(rm4, hit[LAST - 1][:, 0:E + 16].indirect(T.lk4[:]), F.Copy),
            ["hit%d" % (LAST - 1), "hpad%d" % (LAST - 1), "lk4", "part%d" % LAST], [rmk], G1, 0)
    turned(T.m1, "m1", T.part, LAST, i15, ["id2", "part%d" % LAST], True)
    mm(T.m1[:], col(T.dm, LAST - 1, 128), rm4, False, False, ["dm", rmk], "m1", 0)
    todo = list(range(RO + ahead, 16)) + [i for i in range(LAST) if i != r]
    if r < LAST:
        mm(fb, hw, T.ok[:], True, False, ["hw", "ok", "relv"], fk, 2)
    else:
        mm(fb, ident, col(T.eq, RO), True, False, ["eq%d" % RO, "relv"], fk, 2)

    def acc(w, x, R, stop=False, pr=2):
        mms([(fb, w, x, False, stop)], R + ([] if stop else [fk]), [fk] if stop else [], pr)

    def differ(i, n):
        bank, key = banks[n % 2] if n < M3 else banks[n % 3]
        mms([(bank, md, col(T.zall, i), True, i >= LAST)] + ([(bank, g32, col(T.rem, 2 * i + 1), False, True)] if i < LAST else []),
            ["md", "zall", "id6", "relv"] + (["rem%d" % (2 * i + 1)] if i < LAST else []), [key])
        return bank, key

    for i in range(RO + 1, RO + ahead):
        acc(ident, col(T.eq, i), ["eq%d" % i])
    if r < LAST:
        acc(n256i, T.eqs[:], ["id3", "eqs"])
        bank4, key4 = differ(LAST, 1)
        vop(lambda: ve.tensor_scalar(col(T.eq, LAST), bank4, 0.0, None, A.is_equal), [], ["eq%d" % LAST, key4], E, 2)
        acc(ident, col(T.eq, LAST), ["eq%d" % LAST])
    for n, i in enumerate(todo):
        bank, key = differ(i, n); c = n % 4
        if n < 2:
            vop(lambda bank=bank, c=c: ve.tensor_copy(col(T.eq, c), bank), [], ["eq%d" % c, key], E, 2)
        else:
            vop(lambda bank=bank, c=c: ve.tensor_tensor(col(T.eq, c), col(T.eq, c ^ 2), bank, A.mult), ["eq%d" % (c ^ 2)], ["eq%d" % c, key], E, 2)
        if i < LAST:
            acc(col(T.dm, i, 128), col(T.rem, 2 * i), ["dm", "rem%d" % (2 * i)])
    for n in (len(todo) - 2, len(todo) - 1):
        c = n % 4
        vop(lambda c=c: ve.tensor_scalar(col(T.eq, c ^ 2), col(T.eq, c), 0.0, None, A.is_equal), ["eq%d" % c], ["eq%d" % (c ^ 2)], E // 2, 2)
        acc(p32i, col(T.eq, c ^ 2), ["id5", "eq%d" % (c ^ 2)])
    decide(LAST, col(T.pb0, 1), "pb0_1", T.red[:], "red")
    if r == LAST:
        acc(hw, T.ok[:], ["hw", "ok"], False, 0)
        acc(n256i, T.eqs[:], ["id3", "eqs"], True, 0)
    else:
        rem(LAST, 0)
        vop(lambda: ve.tensor_copy(col(T.eq, RO), hit[LAST][:, 0:E + 16].indirect(col(T.lkl, 2 * LAST + 1, 32))),
            ["hit%d" % LAST, "hpad%d" % LAST, "lkl"], ["eq%d" % RO], G1, -1)
        acc(col(T.dm, LAST, 128), col(T.rem, 2 * LAST), ["dm", "rem%d" % (2 * LAST)], False, 0)
        acc(ngm, col(T.eq, RO), ["ngm", "eq%d" % RO], True, 0)
    vop(lambda: ve.tensor_scalar(T.flag[:], fb, 128.5, None, A.is_gt), [], ["flag", fk], E, -1)
    dma("sy", "dfl", [(T.yflag[:], T.flag[:])], ["flag"], [])
    for k in range(LAST):
        if k != r:
            dma("sy", "do%d" % k, [(T.ysep[:, k * E:(k + 1) * E], col(T.sepc, k, 32))], ["sepc%d" % k], [])
    return ops


def order(ranks):
    ext = {}
    for ops in ranks:
        next(o for o in ops if o["sends"])["cost"] += 2500
        for o in ops:
            o["next"] = []
            for k, keys, sem, n in o["sends"]:
                for key in keys:
                    ext[(k, key)] = o
    cand = {}
    for r, ops in enumerate(ranks):
        lw = {}; rd = {}
        for n, o in enumerate(ops):
            pre = {}
            for k in o["R"] + o["W"]:
                p = lw.get(k) or ext.get((r, k))
                if p is not None:
                    pre[(p["r"], p.get("n", -1), k if p["r"] != r else "")] = p
            for k in o["W"]:
                for p in rd.get(k, []):
                    pre[(r, p["n"], "")] = p
            o["n"] = n; o["left"] = len(pre); o["ready"] = 0.0
            o["key"] = (round(o["pr"]), n + 100 * (o["pr"] - round(o["pr"])))
            for p in pre.values():
                p["next"].append(o)
            for k in o["R"]:
                rd.setdefault(k, []).append(o)
            for k in o["W"]:
                lw[k] = o; rd[k] = []
            cand.setdefault((r, o["q"]), [])
            if not pre:
                cand[(r, o["q"])].append(o)
    free = {q: 0.0 for q in cand}; out = [[] for _ in ranks]; pick = {}
    while True:
        for q, c in cand.items():
            if q not in pick and c:
                t0 = max(free[q], min(o["ready"] for o in c))
                o = min((o for o in c if o["ready"] <= t0 + (SLACK if o["pr"] > 0 else URGENT)), key=lambda o: o["key"])
                pick[q] = (max(t0, o["ready"]), o)
        if not pick:
            return out
        q = min(pick, key=lambda q: pick[q][0]); t, o = pick.pop(q)
        cand[q].remove(o); out[q[0]].append(o); free[q] = t + o["cost"]
        for x in o["next"]:
            x["ready"] = max(x["ready"], free[q] + (0 if q == (x["r"], "pe") and x["q"] == "pe" else o["lat"] + HOP))
            x["left"] -= 1
            if x["left"] == 0:
                cand[(x["r"], x["q"])].append(x); pick.pop((x["r"], x["q"]), None)


def rank_program(g, core, T, topo):
    r = T.rank_of(core)
    if r is None:
        return
    ranks = [build(k, g, T, topo) for k in range(N)]
    if not PLAN:
        PLAN.extend([o["n"] for o in ops] for ops in order(ranks))
    Q = {"ve": g.vector, "ac": g.scalar, "pe": g.tensor, "po": g, "sy": g.sync}
    cnt = {}; waited = {q: {} for q in Q}; lw = {}; rd = {}
    mine = [s for ops in ranks for o in ops for s in o["sends"] if s[0] == r]
    for k, keys, sem, n in mine:
        cnt[sem] = cnt.get(sem, 0) + n
    for k, keys, sem, n in mine:
        for key in keys:
            lw[key] = (sem, cnt[sem])

    def need(q, tok):
        if not (q == "pe" and tok[0] == "pe") and waited[q].get(tok[0], 0) < tok[1]:
            Q[q].wait_ge(T.sem[tok[0]], tok[1]); waited[q][tok[0]] = tok[1]

    for o in [ranks[r][n] for n in PLAN[r]]:
        if not o["fns"]:
            continue
        q = o["q"]; best = {}
        for tok in [lw.get(k) for k in o["R"] + o["W"]] + [t for k in o["W"] for t in rd.get(k, [])]:
            if tok is not None and best.get(tok[0], 0) < tok[1]:
                best[tok[0]] = tok[1]
        for s in best:
            need(q, (s, best[s]))
        sem = o["sem"] or q
        for fn in o["fns"]:
            if sem == "ls":
                fn(); cnt[sem] = cnt.get(sem, 0) + sum(s[3] for s in o["sends"])
            else:
                n = 16 if o["sem"] else 1
                fn().then_inc(T.sem[sem], n); cnt[sem] = cnt.get(sem, 0) + n
        tok = (sem, cnt[sem])
        for k in o["R"]:
            rd.setdefault(k, []).append(tok)
        for k in o["W"]:
            lw[k] = tok; rd[k] = []
    for s in cnt:
        need("po", (s, cnt[s]))
